import numpy as np
import ml_dtypes


def mxq(x, axis, fmt="e4m3"):
    dtype, down = {"e4m3": (ml_dtypes.float8_e4m3fn, 7), "e5m2": (ml_dtypes.float8_e5m2, 14)}[fmt]
    v = np.moveaxis(np.asarray(x, np.float32).astype(ml_dtypes.bfloat16).astype(np.float64), axis, -1)
    blocks = v.reshape(v.shape[:-1] + (-1, 32))
    amax = np.abs(blocks).max(-1, keepdims=True)
    byte = np.maximum(np.where(amax > 0, np.frexp(amax)[1] - 1 + 127, 0) - down, 1)
    scale = np.exp2(byte - 127.0)
    codes = (blocks / scale).astype(np.float32).astype(dtype).astype(np.float64)
    return np.moveaxis((codes * scale).reshape(v.shape), -1, axis)


WIDE = False


def mx_kscale(k):
    if not WIDE:
        return np.ones(k)
    levels = np.array([10, -10, 5, -5, 0])
    if k % 512:
        return np.exp2(np.random.permutation(np.resize(levels, k // 32))).repeat(32)
    a = np.empty((k // 512, 16))
    for p in range(k // 512):
        a[p, :8] = np.random.permutation(np.resize(levels, 8))
        for g in range(8):
            far = levels[np.abs(levels - a[p, g]) >= 10]
            a[p, g + 8] = far[np.random.randint(len(far))]
    return np.exp2(a.ravel()).repeat(32)


def f64(x):
    return np.asarray(x).astype(np.float64)


def striped(idx):
    return np.tile(idx.reshape(-1, 16).T, (8, 1)).astype(np.uint16)


def unstriped(offs):
    return offs[:16].T.reshape(-1).astype(np.int64)


E2M1 = np.array([0.0, 0.5, 1.0, 1.5, 2.0, 3.0, 4.0, 6.0, -0.0, -0.5, -1.0, -1.5, -2.0, -3.0, -4.0, -6.0])


def pack_weight(w, fmt):
    k, n = w.shape
    w = f64(np.asarray(w, np.float32).astype(ml_dtypes.bfloat16)).reshape(k // 32, 32, n)
    amax = np.abs(w).max(1)
    if fmt == "e4m3":
        byte = np.frexp(amax)[1] - 1 + 127 - 7
    else:
        mant, ex = np.frexp(amax / 6.0)
        byte = np.where(mant > 0.5, ex, ex - 1) + 127
    byte = np.clip(np.where(amax > 0, byte, 1), 1, 254)
    scaled = (w * np.exp2(127.0 - byte)[:, None, :]).reshape(k, n).astype(np.float32)
    by_word = np.ascontiguousarray(scaled.reshape(k // 512, 128, 4, n).transpose(0, 1, 3, 2))
    if fmt == "e4m3":
        words = by_word.astype(ml_dtypes.float8_e4m3fn).view(np.uint8)
    else:
        c = by_word.astype(ml_dtypes.float4_e2m1fn).view(np.uint8) & 0xF
        words = (c[..., 0::2] | (c[..., 1::2] << 4)).reshape(k // 512, 128, 2 * n)
    return np.ascontiguousarray(words), np.ascontiguousarray(byte.astype(np.uint8).reshape(k // 512, 16, n))


def unpack_weight(words, scales, fmt):
    g, _, n = scales.shape
    words = np.ascontiguousarray(words).reshape(g, 128, n, -1)
    if fmt == "e4m3":
        vals = words.view(ml_dtypes.float8_e4m3fn).astype(np.float64)
    else:
        nib = np.empty((g, 128, n, 4), np.uint8)
        nib[..., 0::2] = words & 0xF
        nib[..., 1::2] = words >> 4
        vals = E2M1[nib]
    vals = vals * np.repeat(np.exp2(scales.astype(np.float64) - 127.0), 8, axis=1)[..., None]
    return vals.transpose(0, 1, 3, 2).reshape(g * 512, n)


K, T, E, N = 2560, 768, 6, 128
COUNTS = (128, 128, 128, 256, 384, 512)
STARTS = np.cumsum((0,) + COUNTS)


def by_expert(wq, xq):
    return np.concatenate([wq[e].T @ xq[:, STARTS[e]:STARTS[e + 1]] for e in range(E)], axis=1)


def setup_inputs():
    n = np.random.standard_normal
    s = mx_kscale(K)[:, None]
    both = np.repeat(np.arange(E), COUNTS)
    pair = np.stack([both[:T], both[T:]])[:, np.random.permutation(T)]
    pair = np.where(np.random.rand(T) < 0.5, pair, pair[::-1])
    order = np.argsort(pair.reshape(-1), kind="stable")
    slot_token = order % T; pos = np.empty(2 * T, np.int64); pos[order] = np.arange(2 * T); pos = pos.reshape(2, T)
    g = np.random.uniform(0.2, 0.8, T)
    w = [pack_weight(m, "e2m1") for m in n((E, K, N)) / np.sqrt(K) / s[None]]
    return {
        "xT": (n((K, T)) * s).astype(np.float32),
        "w_words": np.stack([m[0] for m in w]),
        "w_scales": np.stack([m[1] for m in w]),
        "b": (0.3 * n((N, E))).astype(np.float32),
        "gate": np.stack([np.tile(g, (N, 1)), np.tile(1.0 - g, (N, 1))]).astype(np.float32),
        "offs": striped(slot_token),
        "pos1": striped(pos[0]),
        "pos2": striped(pos[1]),
    }


def reference(xT, w_words, w_scales, b, gate, offs, pos1, pos2):
    idx = unstriped(offs)
    w = np.stack([unpack_weight(w_words[e], w_scales[e], "e2m1") for e in range(E)])
    xq = mxq(f64(xT)[:, idx], 0, "e4m3")
    y = by_expert(w, xq)
    y = y + np.repeat(f64(b), COUNTS, axis=1)
    return f64(gate[0]) * y[:, unstriped(pos1)] + f64(gate[1]) * y[:, unstriped(pos2)]

@@ -1,0 +1,226 @@
+from contextlib import ExitStack
+
+import concourse.mybir as mybir
+
+FLOPS = 2 * 1536 * 2560 * 128
+
+F32 = mybir.dt.float32
+BF16 = mybir.dt.bfloat16
+I32 = mybir.dt.int32
+U32 = mybir.dt.uint32
+U16 = mybir.dt.uint16
+U8 = mybir.dt.uint8
+FP8X4 = mybir.dt.float8_e4m3fn_x4
+FP4X4 = mybir.dt.float4_e2m1fn_x4
+MULT = mybir.AluOpType.mult
+IDENTITY = mybir.ActivationFunctionType.Identity
+
+P = 128
+T = 768
+S = 1536
+E = 6
+N = 128
+A = 5
+
+
+def tile_moe_rag_lin_bias_kernel(tc, xT, w_words, w_scales, b, gate, offs, pos1, pos2, out):
+    nc = tc.nc
+    with ExitStack() as ctx:
+        pool = ctx.enter_context(tc.tile_pool(name="held", bufs=1))
+        psum = ctx.enter_context(tc.psum_pool(name="psum", bufs=1))
+
+        def held(shape, dtype, name):
+            return pool.tile(shape, dtype, name=name, align_bytes=64)
+
+        offs_t = held([P, S // 16], U16, "offs_t")
+        pos1_t = held([P, T // 16], U16, "pos1_t")
+        pos2_t = held([P, T // 16], U16, "pos2_t")
+
+        chunks = [
+            [(0, 256, "v"), (256, 256, "s"), (512, 128, "v"), (640, 128, "s")],
+            [(0, 512, "s"), (512, 256, "v")],
+            [(0, 512, "s"), (512, 256, "s")],
+            [(0, 512, "s"), (512, 256, "s")],
+            [(0, 512, "s"), (512, 256, "s")],
+        ]
+        loads = [((0, 512), (512, 768)), ((0, 768),), ((0, 768),), ((0, 768),), ((0, 512), (512, 768))]
+
+        nc.sync.dma_start(offs_t[:], offs)
+        raws = {}
+
+        def load(a):
+            rows = xT[512 * a : 512 * (a + 1), :].rearrange("(p j) w -> p j w", j=4)
+            for t0, t1 in loads[a]:
+                raw = held([P, 4, t1 - t0], F32, "raw_%d_%d" % (a, t0))
+                nc.sync.dma_start(out=raw[:], in_=rows[:, :, t0:t1])
+                for c0, cn, eng in chunks[a]:
+                    if t0 <= c0 < t1:
+                        raws[(a, c0)] = raw[:, :, c0 - t0 : c0 - t0 + cn]
+
+        for a in range(4):
+            load(a)
+
+        words = held([P, E * A * 2 * N], U8, "words")
+        wplane = held([P, E * A * N], U8, "wplane")
+        lone = held([P, T], U8, "lone")
+        packed = held([P, T], U8, "packed")
+        moved = {}
+        for a in (1, 2, 3):
+            moved[a] = held([P, S], U8, "moved_%d" % a)
+        for plane in (packed, lone, wplane, moved[1], moved[2], moved[3]):
+            nc.gpsimd.memset(plane[:].bitcast(I32), 0)
+
+        b_t = held([P, E], F32, "b_t")
+        nc.sync.dma_start(out=b_t[:], in_=b)
+        for q in range(4):
+            nc.sync.dma_start(
+                out=wplane[32 * q : 32 * q + 4, :].bitcast(I32).rearrange("r (m c) -> r m c", m=E * A),
+                in_=w_scales[:, :, 4 * q : 4 * q + 4, :].bitcast(I32).rearrange("e a r c -> r (e a) c"),
+            )
+        for e0, e1 in ((3, 6), (0, 3)):
+            nc.sync.dma_start(
+                out=words[:, 2 * N * A * e0 : 2 * N * A * e1].bitcast(I32).rearrange("p (m c) -> p m c", c=N // 2),
+                in_=w_words[e0:e1].bitcast(I32).rearrange("e a p c -> p (e a) c"),
+            )
+            if e0 == 3:
+                load(4)
+        gates = []
+        for c in range(2):
+            g_t = held([P, T], F32, "gate_%d" % c)
+            nc.sync.dma_start(out=g_t[:], in_=gate[c])
+            gates.append(g_t)
+        nc.sync.dma_start(pos1_t[:], pos1)
+        nc.sync.dma_start(pos2_t[:], pos2)
+
+        codes = {}
+        gwords = {}
+        for a in range(A):
+            codes[a] = held([P, T], U32, "codes_%d" % a)
+            gwords[a] = held([P, S], U32, "gwords_%d" % a)
+        glone = held([P, S], U8, "glone")
+        gpacked = held([P, S], U8, "gpacked")
+
+        groups = {}
+
+        def cast(a):
+            for t0, tn, eng in chunks[a]:
+                grouped = held([P, tn, 4], BF16, "grouped_%d_%d" % (a, t0))
+                src = raws[(a, t0)].rearrange("p j w -> p w j")
+                if eng == "v":
+                    nc.vector.tensor_copy(out=grouped[:], in_=src)
+                else:
+                    nc.scalar.copy(out=grouped[:], in_=src)
+                groups[(a, t0)] = grouped
+
+        def quantize(a):
+            for t0, tn, eng in chunks[a]:
+                plane = lone[:, t0 : t0 + tn] if a == A - 1 else packed[4 * a : P, t0 : t0 + tn]
+                nc.vector.quantize_mx(
+                    out=codes[a][:, t0 : t0 + tn].bitcast(FP8X4),
+                    scales=plane,
+                    in_=groups[(a, t0)][:].rearrange("p w j -> p (w j)"),
+                )
+
+        def gather(dst, src, s0, s1):
+            nc.vector.tensor_copy(dst[:, s0:s1], src[:].indirect(offs_t[:, s0 // 16 : s1 // 16]))
+
+        planes = {0: gpacked, 1: moved[1], 2: moved[2], 3: moved[3], 4: glone}
+
+        blocks = [
+            (7, 0, 5, 1024, 512),
+            (4, 0, 3, 512, 128),
+            (5, 0, 4, 640, 128),
+            (6, 0, 4, 768, 128),
+            (6, 128, 4, 896, 128),
+            (1, 0, 1, 128, 128),
+            (2, 0, 2, 256, 128),
+            (3, 0, 3, 384, 128),
+            (0, 0, 0, 0, 128),
+        ]
+        early = [blk for blk in blocks if blk[1] == 0]
+        banks = []
+        for i in range(8):
+            banks.append(psum.tile([P, 512], F32, name="bank_%d" % i))
+        y = held([P, S], F32, "y")
+
+        def multiply(a, block):
+            bank, col, e, s0, sn = block
+            m = e * A + a
+            nc.tensor.matmul_mx(
+                out=banks[bank][:, col : col + sn],
+                lhsT=words[:, 2 * N * m : 2 * N * (m + 1)].bitcast(FP4X4),
+                lhsT_scale=wplane[:, N * m : N * (m + 1)],
+                rhs=gwords[a][:, s0 : s0 + sn].bitcast(FP8X4),
+                rhs_scale=planes[a][:, s0 : s0 + sn],
+                start=(a == 0),
+                stop=(a == A - 1),
+            )
+
+        def leave(bank, col, e, s0, sn):
+            if s0 == 0:
+                nc.vector.tensor_scalar_add(out=y[:, s0 : s0 + sn], in0=banks[bank][:, col : col + sn], scalar1=b_t[:, e : e + 1])
+            else:
+                nc.scalar.activation(out=y[:, s0 : s0 + sn], in_=banks[bank][:, col : col + sn], func=IDENTITY, bias=b_t[:, e : e + 1])
+
+        thirds = ((0, 512), (512, 1024), (1024, 1536))
+
+        cast(0)
+        cast(1)
+        quantize(0)
+        for s0, s1 in thirds:
+            gather(gwords[0], codes[0], s0, s1)
+        cast(2)
+        quantize(1)
+        for s0, s1 in thirds:
+            gather(gwords[1], codes[1], s0, s1)
+        cast(3)
+        quantize(2)
+        for s0, s1 in thirds:
+            gather(gwords[2], codes[2], s0, s1)
+        cast(4)
+        quantize(3)
+        for s0, s1 in thirds:
+            gather(gpacked, packed, s0, s1)
+        for a in (1, 2, 3):
+            nc.sync.dma_start(out=moved[a][0 : P - 4 * a, :].bitcast(I32), in_=gpacked[4 * a : P, :].bitcast(I32))
+        for s0, s1 in thirds:
+            gather(gwords[3], codes[3], s0, s1)
+        for blk in early:
+            for a in range(4):
+                multiply(a, blk)
+        quantize(4)
+
+        for s0, s1 in ((1024, 1536), (512, 1024), (128, 512), (0, 128)):
+            gather(glone, lone, s0, s1)
+            gather(gwords[4], codes[4], s0, s1)
+            for blk in blocks:
+                if s0 <= blk[3] < s1:
+                    if blk[1] > 0:
+                        for a in range(A - 1):
+                            multiply(a, blk)
+                    multiply(4, blk)
+                    if blk[0] == 6:
+                        if blk[1] > 0:
+                            leave(6, 0, 4, 768, 256)
+                    else:
+                        leave(*blk)
+
+        terms = {}
+
+        def fetch(c, t0, t1):
+            pos = (pos1_t, pos2_t)[c]
+            term = held([P, t1 - t0], F32, "term_%d_%d" % (c, t0))
+            nc.vector.tensor_tensor(term[:], y[:].indirect(pos[:, t0 // 16 : t1 // 16]), gates[c][:, t0:t1], MULT)
+            terms[(c, t0)] = term
+
+        def finish(t0, t1):
+            total = held([P, t1 - t0], F32, "total_%d" % t0)
+            nc.vector.tensor_add(out=total[:], in0=terms[(0, t0)][:], in1=terms[(1, t0)][:])
+            nc.sync.dma_start(out=out[:, t0:t1], in_=total[:])
+
+        fetch(0, 0, 512)
+        fetch(1, 0, 512)
+        fetch(0, 512, 768)
+        finish(0, 512)
+        fetch(1, 512, 768)
+        finish(512, 768)

@@ -21,6 +21,8 @@ S = 1536
 E = 6
 N = 128
 A = 5
+LAST = 1024
+WINDOW = 2048
 
 
 def tile_moe_rag_lin_bias_kernel(tc, xT, w_words, w_scales, b, gate, offs, pos1, pos2, out):
@@ -29,23 +31,29 @@ def tile_moe_rag_lin_bias_kernel(tc, xT, w_words, w_scales, b, gate, offs, pos1,
         pool = ctx.enter_context(tc.tile_pool(name="held", bufs=1))
         psum = ctx.enter_context(tc.psum_pool(name="psum", bufs=1))
 
-        def held(shape, dtype, name):
-            return pool.tile(shape, dtype, name=name, align_bytes=64)
+        def held(shape, dtype, name, tag=None):
+            return pool.tile(shape, dtype, name=name, tag=tag or name, align_bytes=64)
 
         offs_t = held([P, S // 16], U16, "offs_t")
         pos1_t = held([P, T // 16], U16, "pos1_t")
         pos2_t = held([P, T // 16], U16, "pos2_t")
 
-        chunks = [
-            [(0, 256, "v"), (256, 256, "s"), (512, 128, "v"), (640, 128, "s")],
-            [(0, 512, "s"), (512, 256, "v")],
-            [(0, 512, "s"), (512, 256, "s")],
-            [(0, 512, "s"), (512, 256, "s")],
-            [(0, 512, "s"), (512, 256, "s")],
+        loads = [
+            ((0, 512), (512, 768)),
+            ((0, 256), (256, 512), (512, 768)),
+            ((0, 256), (256, 512), (512, 768)),
+            ((0, 512), (512, 768)),
+            ((0, 512), (512, 768)),
         ]
-        loads = [((0, 512), (512, 768)), ((0, 768),), ((0, 768),), ((0, 768),), ((0, 512), (512, 768))]
+        casts = [
+            ((0, 320, "v"), (320, 512, "s"), (512, 672, "v"), (672, 768, "s")),
+            ((0, 256, "s"), (256, 512, "s"), (512, 768, "s")),
+            ((0, 256, "s"), (256, 512, "s"), (512, 768, "s")),
+            ((0, 512, "s"), (512, 768, "s")),
+            ((0, 512, "s"), (512, 768, "s")),
+        ]
+        quants = ((0, 512), (512, 768))
 
-        nc.sync.dma_start(offs_t[:], offs)
         raws = {}
 
         def load(a):
@@ -53,91 +61,111 @@ def tile_moe_rag_lin_bias_kernel(tc, xT, w_words, w_scales, b, gate, offs, pos1,
             for t0, t1 in loads[a]:
                 raw = held([P, 4, t1 - t0], F32, "raw_%d_%d" % (a, t0))
                 nc.sync.dma_start(out=raw[:], in_=rows[:, :, t0:t1])
-                for c0, cn, eng in chunks[a]:
+                for c0, c1, eng in casts[a]:
                     if t0 <= c0 < t1:
-                        raws[(a, c0)] = raw[:, :, c0 - t0 : c0 - t0 + cn]
+                        raws[(a, c0)] = raw[:, :, c0 - t0 : c1 - t0]
 
-        for a in range(4):
+        load(0)
+        nc.sync.dma_start(offs_t[:], offs)
+        nc.sync.dma_start(pos1_t[:], pos1)
+        nc.sync.dma_start(pos2_t[:], pos2)
+        b_t = held([P, E], F32, "b_t")
+        nc.sync.dma_start(out=b_t[:], in_=b)
+        for a in range(1, A):
             load(a)
 
         words = held([P, E * A * 2 * N], U8, "words")
         wplane = held([P, E * A * N], U8, "wplane")
-        lone = held([P, T], U8, "lone")
-        packed = held([P, T], U8, "packed")
+        packed = held([P, WINDOW], U8, "packed")
+        codes = held([P, (A - 1) * T + WINDOW], U32, "codes")
+        nc.gpsimd.memset(codes[:, A * T :].bitcast(I32), 0)
         moved = {}
         for a in (1, 2, 3):
-            moved[a] = held([P, S], U8, "moved_%d" % a)
-        for plane in (packed, lone, wplane, moved[1], moved[2], moved[3]):
+            moved[a] = held([P, LAST], U8, "moved_%d" % a)
+        late = {}
+        for a in (1, 2, 3, 4):
+            late[a] = held([P, S - LAST], U8, "late_%d" % a)
+        for plane in (packed, wplane, moved[1], moved[2], moved[3], late[1], late[2], late[3]):
             nc.gpsimd.memset(plane[:].bitcast(I32), 0)
 
-        b_t = held([P, E], F32, "b_t")
-        nc.sync.dma_start(out=b_t[:], in_=b)
         for q in range(4):
             nc.sync.dma_start(
                 out=wplane[32 * q : 32 * q + 4, :].bitcast(I32).rearrange("r (m c) -> r m c", m=E * A),
                 in_=w_scales[:, :, 4 * q : 4 * q + 4, :].bitcast(I32).rearrange("e a r c -> r (e a) c"),
             )
-        for e0, e1 in ((3, 6), (0, 3)):
+        for e0, e1 in ((0, 3), (3, 6)):
             nc.sync.dma_start(
                 out=words[:, 2 * N * A * e0 : 2 * N * A * e1].bitcast(I32).rearrange("p (m c) -> p m c", c=N // 2),
                 in_=w_words[e0:e1].bitcast(I32).rearrange("e a p c -> p (e a) c"),
             )
-            if e0 == 3:
-                load(4)
-        gates = []
-        for c in range(2):
-            g_t = held([P, T], F32, "gate_%d" % c)
-            nc.sync.dma_start(out=g_t[:], in_=gate[c])
-            gates.append(g_t)
-        nc.sync.dma_start(pos1_t[:], pos1)
-        nc.sync.dma_start(pos2_t[:], pos2)
 
-        codes = {}
         gwords = {}
-        for a in range(A):
-            codes[a] = held([P, T], U32, "codes_%d" % a)
+        for a in range(3):
             gwords[a] = held([P, S], U32, "gwords_%d" % a)
-        glone = held([P, S], U8, "glone")
-        gpacked = held([P, S], U8, "gpacked")
+        gearly = held([P, S], U8, "gearly")
+        glate = held([P, LAST], U8, "glate")
 
         groups = {}
 
         def cast(a):
-            for t0, tn, eng in chunks[a]:
-                grouped = held([P, tn, 4], BF16, "grouped_%d_%d" % (a, t0))
-                src = raws[(a, t0)].rearrange("p j w -> p w j")
+            for t0, t1 in quants:
+                groups[(a, t0)] = held([P, t1 - t0, 4], BF16, "grouped_%d_%d" % (a, t0))
+            for c0, c1, eng in casts[a]:
+                t0 = 0 if c0 < 512 else 512
+                dst = groups[(a, t0)][:, c0 - t0 : c1 - t0, :]
+                src = raws[(a, c0)].rearrange("p j w -> p w j")
                 if eng == "v":
-                    nc.vector.tensor_copy(out=grouped[:], in_=src)
+                    nc.vector.tensor_copy(out=dst, in_=src)
                 else:
-                    nc.scalar.copy(out=grouped[:], in_=src)
-                groups[(a, t0)] = grouped
+                    nc.scalar.copy(out=dst, in_=src)
 
         def quantize(a):
-            for t0, tn, eng in chunks[a]:
-                plane = lone[:, t0 : t0 + tn] if a == A - 1 else packed[4 * a : P, t0 : t0 + tn]
+            for t0, t1 in quants:
                 nc.vector.quantize_mx(
-                    out=codes[a][:, t0 : t0 + tn].bitcast(FP8X4),
-                    scales=plane,
+                    out=codes[:, (A - 1 - a) * T + t0 : (A - 1 - a) * T + t1].bitcast(FP8X4),
+                    scales=packed[4 * (a % 4) : P, t0:t1],
                     in_=groups[(a, t0)][:].rearrange("p w j -> p (w j)"),
                 )
 
         def gather(dst, src, s0, s1):
-            nc.vector.tensor_copy(dst[:, s0:s1], src[:].indirect(offs_t[:, s0 // 16 : s1 // 16]))
+            nc.vector.tensor_copy(dst, src.indirect(offs_t[:, s0 // 16 : s1 // 16]))
 
-        planes = {0: gpacked, 1: moved[1], 2: moved[2], 3: moved[3], 4: glone}
+        def gather_words(dst, a, s0, s1):
+            first = (A - 1 - a) * T
+            gather(dst, codes[:, first : first + (WINDOW if s1 - s0 > 512 else T)], s0, s1)
+
+        def gather_bytes(dst, s0, s1):
+            gather(dst, packed[:, 0 : (WINDOW if s1 - s0 > 512 else T)], s0, s1)
+
+        def slot_words(a, s0, sn):
+            if a == 3:
+                return g3_last[:, s0 - LAST : s0 - LAST + sn] if s0 >= LAST else g3_rest[0][:, s0 : s0 + sn]
+            if a == 4 and s0 >= LAST:
+                return g4_last[:, s0 - LAST : s0 - LAST + sn]
+            return gwords[a][:, s0 : s0 + sn]
+
+        def slot_plane(a, s0, sn):
+            if a == 0:
+                return gearly[:, s0 : s0 + sn]
+            if s0 >= LAST:
+                return late[a][:, s0 - LAST : s0 - LAST + sn]
+            return moved[a][:, s0 : s0 + sn] if a < 4 else glate[:, s0 : s0 + sn]
+
+        g3_last = held([P, S - LAST], U32, "g3_last")
+        g4_last = held([P, S - LAST], U32, "g4_last")
+        g3_rest = []
 
         blocks = [
-            (7, 0, 5, 1024, 512),
-            (4, 0, 3, 512, 128),
-            (5, 0, 4, 640, 128),
             (6, 0, 4, 768, 128),
             (6, 128, 4, 896, 128),
+            (5, 0, 4, 640, 128),
+            (4, 0, 3, 512, 128),
             (1, 0, 1, 128, 128),
             (2, 0, 2, 256, 128),
             (3, 0, 3, 384, 128),
+            (7, 0, 5, 1024, 512),
             (0, 0, 0, 0, 128),
         ]
-        early = [blk for blk in blocks if blk[1] == 0]
         banks = []
         for i in range(8):
             banks.append(psum.tile([P, 512], F32, name="bank_%d" % i))
@@ -150,8 +178,8 @@ def tile_moe_rag_lin_bias_kernel(tc, xT, w_words, w_scales, b, gate, offs, pos1,
                 out=banks[bank][:, col : col + sn],
                 lhsT=words[:, 2 * N * m : 2 * N * (m + 1)].bitcast(FP4X4),
                 lhsT_scale=wplane[:, N * m : N * (m + 1)],
-                rhs=gwords[a][:, s0 : s0 + sn].bitcast(FP8X4),
-                rhs_scale=planes[a][:, s0 : s0 + sn],
+                rhs=slot_words(a, s0, sn).bitcast(FP8X4),
+                rhs_scale=slot_plane(a, s0, sn),
                 start=(a == 0),
                 stop=(a == A - 1),
             )
@@ -162,37 +190,46 @@ def tile_moe_rag_lin_bias_kernel(tc, xT, w_words, w_scales, b, gate, offs, pos1,
             else:
                 nc.scalar.activation(out=y[:, s0 : s0 + sn], in_=banks[bank][:, col : col + sn], func=IDENTITY, bias=b_t[:, e : e + 1])
 
-        thirds = ((0, 512), (512, 1024), (1024, 1536))
-
         cast(0)
         cast(1)
         quantize(0)
-        for s0, s1 in thirds:
-            gather(gwords[0], codes[0], s0, s1)
+        gather_bytes(gearly[:, LAST:S], LAST, S)
+        gather_words(gwords[0][:], 0, 0, S)
         cast(2)
         quantize(1)
-        for s0, s1 in thirds:
-            gather(gwords[1], codes[1], s0, s1)
+        gather_words(gwords[1][:], 1, 0, S)
         cast(3)
         quantize(2)
-        for s0, s1 in thirds:
-            gather(gwords[2], codes[2], s0, s1)
+        gather_words(gwords[2][:], 2, 0, S)
         cast(4)
         quantize(3)
-        for s0, s1 in thirds:
-            gather(gpacked, packed, s0, s1)
+        gather_bytes(gearly[:, 0:LAST], 0, LAST)
         for a in (1, 2, 3):
-            nc.sync.dma_start(out=moved[a][0 : P - 4 * a, :].bitcast(I32), in_=gpacked[4 * a : P, :].bitcast(I32))
-        for s0, s1 in thirds:
-            gather(gwords[3], codes[3], s0, s1)
-        for blk in early:
-            for a in range(4):
-                multiply(a, blk)
+            nc.sync.dma_start(out=moved[a][0 : P - 4 * a, :].bitcast(I32), in_=gearly[4 * a : P, 0:LAST].bitcast(I32))
+        gather_words(g3_last[:], 3, LAST, S)
+        for blk in blocks:
+            if blk[1] == 0:
+                for a in range(1 if blk[3] == LAST else 3):
+                    multiply(a, blk)
         quantize(4)
+        gates = held([P, 2, T], F32, "gates", tag="grouped_4_0")
+        nc.sync.dma_start(out=gates[:], in_=gate.rearrange("c p t -> p c t"))
+        glast = held([P, S - LAST], U8, "glast")
+        gather_bytes(glast[:], LAST, S)
+        for a in (1, 2, 3):
+            nc.sync.dma_start(out=late[a][0 : P - 4 * a, :].bitcast(I32), in_=glast[4 * a : P, :].bitcast(I32))
+        nc.sync.dma_start(out=late[4][:].bitcast(I32), in_=glast[:].bitcast(I32))
+        g3_rest.append(held([P, LAST], U32, "g3_rest", tag="grouped_4_512"))
+        gather_words(g3_rest[0][:], 3, 0, LAST)
+        for blk in blocks:
+            if blk[1] == 0:
+                for a in range(1 if blk[3] == LAST else 3, 4):
+                    multiply(a, blk)
+        gather_bytes(glate[:], 0, LAST)
+        gwords[4] = held([P, LAST], U32, "gwords_4", tag="glast")
 
-        for s0, s1 in ((1024, 1536), (512, 1024), (128, 512), (0, 128)):
-            gather(glone, lone, s0, s1)
-            gather(gwords[4], codes[4], s0, s1)
+        for s0, s1 in ((1024, 1536), (640, 1024), (128, 640), (0, 128)):
+            gather_words(g4_last[:] if s0 == LAST else gwords[4][:, s0:s1], 4, s0, s1)
             for blk in blocks:
                 if s0 <= blk[3] < s1:
                     if blk[1] > 0:
@@ -210,7 +247,7 @@ def tile_moe_rag_lin_bias_kernel(tc, xT, w_words, w_scales, b, gate, offs, pos1,
         def fetch(c, t0, t1):
             pos = (pos1_t, pos2_t)[c]
             term = held([P, t1 - t0], F32, "term_%d_%d" % (c, t0))
-            nc.vector.tensor_tensor(term[:], y[:].indirect(pos[:, t0 // 16 : t1 // 16]), gates[c][:, t0:t1], MULT)
+            nc.vector.tensor_tensor(term[:], y[:].indirect(pos[:, t0 // 16 : t1 // 16]), gates[:, c, t0:t1], MULT)
             terms[(c, t0)] = term
 
         def finish(t0, t1):

@@ -22,6 +22,8 @@ E = 6
 N = 128
 A = 5
 LAST = 1024
+SHIFTED = 112
+HELD = 512
 WINDOW = 2048
 
 
@@ -71,14 +73,14 @@ def tile_moe_rag_lin_bias_kernel(tc, xT, w_words, w_scales, b, gate, offs, pos1,
         nc.sync.dma_start(pos2_t[:], pos2)
         b_t = held([P, E], F32, "b_t")
         nc.sync.dma_start(out=b_t[:], in_=b)
-        for a in range(1, A):
+        for a in range(1, A - 1):
             load(a)
 
         words = held([P, E * A * 2 * N], U8, "words")
         wplane = held([P, E * A * N], U8, "wplane")
         packed = held([P, WINDOW], U8, "packed")
         codes = held([P, (A - 1) * T + WINDOW], U32, "codes")
-        nc.gpsimd.memset(codes[:, A * T :].bitcast(I32), 0)
+        nc.vector.memset(codes[:, A * T :].bitcast(I32), 0)
         moved = {}
         for a in (1, 2, 3):
             moved[a] = held([P, LAST], U8, "moved_%d" % a)
@@ -86,14 +88,16 @@ def tile_moe_rag_lin_bias_kernel(tc, xT, w_words, w_scales, b, gate, offs, pos1,
         for a in (1, 2, 3, 4):
             late[a] = held([P, S - LAST], U8, "late_%d" % a)
         for plane in (packed, wplane, moved[1], moved[2], moved[3], late[1], late[2], late[3]):
-            nc.gpsimd.memset(plane[:].bitcast(I32), 0)
+            nc.vector.memset(plane[:].bitcast(I32), 0)
 
-        for q in range(4):
-            nc.sync.dma_start(
-                out=wplane[32 * q : 32 * q + 4, :].bitcast(I32).rearrange("r (m c) -> r m c", m=E * A),
-                in_=w_scales[:, :, 4 * q : 4 * q + 4, :].bitcast(I32).rearrange("e a r c -> r (e a) c"),
-            )
-        for e0, e1 in ((0, 3), (3, 6)):
+        nc.sync.dma_start(
+            out=wplane[0:16, :].bitcast(I32).rearrange("r (m c) -> r m c", m=E * A),
+            in_=w_scales.bitcast(I32).rearrange("e a r c -> r (e a) c"),
+        )
+        load(A - 1)
+        for q in range(1, 4):
+            nc.sync.dma_start(out=wplane[32 * q : 32 * q + 4, :].bitcast(I32), in_=wplane[4 * q : 4 * q + 4, :].bitcast(I32))
+        for e0, e1 in ((3, 6), (0, 3)):
             nc.sync.dma_start(
                 out=words[:, 2 * N * A * e0 : 2 * N * A * e1].bitcast(I32).rearrange("p (m c) -> p m c", c=N // 2),
                 in_=w_words[e0:e1].bitcast(I32).rearrange("e a p c -> p (e a) c"),
@@ -139,7 +143,7 @@ def tile_moe_rag_lin_bias_kernel(tc, xT, w_words, w_scales, b, gate, offs, pos1,
 
         def slot_words(a, s0, sn):
             if a == 3:
-                return g3_last[:, s0 - LAST : s0 - LAST + sn] if s0 >= LAST else g3_rest[0][:, s0 : s0 + sn]
+                return g3_last[:, s0 - HELD : s0 - HELD + sn] if s0 >= HELD else g3_rest[0][:, s0 : s0 + sn]
             if a == 4 and s0 >= LAST:
                 return g4_last[:, s0 - LAST : s0 - LAST + sn]
             return gwords[a][:, s0 : s0 + sn]
@@ -151,7 +155,7 @@ def tile_moe_rag_lin_bias_kernel(tc, xT, w_words, w_scales, b, gate, offs, pos1,
                 return late[a][:, s0 - LAST : s0 - LAST + sn]
             return moved[a][:, s0 : s0 + sn] if a < 4 else glate[:, s0 : s0 + sn]
 
-        g3_last = held([P, S - LAST], U32, "g3_last")
+        g3_last = held([P, S - HELD], U32, "g3_last")
         g4_last = held([P, S - LAST], U32, "g4_last")
         g3_rest = []
 
@@ -205,27 +209,27 @@ def tile_moe_rag_lin_bias_kernel(tc, xT, w_words, w_scales, b, gate, offs, pos1,
         quantize(3)
         gather_bytes(gearly[:, 0:LAST], 0, LAST)
         for a in (1, 2, 3):
-            nc.sync.dma_start(out=moved[a][0 : P - 4 * a, :].bitcast(I32), in_=gearly[4 * a : P, 0:LAST].bitcast(I32))
-        gather_words(g3_last[:], 3, LAST, S)
+            nc.sync.dma_start(out=moved[a][0:SHIFTED, :].bitcast(I32), in_=gearly[4 * a : 4 * a + SHIFTED, 0:LAST].bitcast(I32))
+        gather_words(g3_last[:], 3, HELD, S)
         for blk in blocks:
             if blk[1] == 0:
-                for a in range(1 if blk[3] == LAST else 3):
+                for a in range(1 if blk[3] == LAST else 4 if blk[3] >= HELD else 3):
                     multiply(a, blk)
         quantize(4)
-        gates = held([P, 2, T], F32, "gates", tag="grouped_4_0")
-        nc.sync.dma_start(out=gates[:], in_=gate.rearrange("c p t -> p c t"))
         glast = held([P, S - LAST], U8, "glast")
         gather_bytes(glast[:], LAST, S)
         for a in (1, 2, 3):
-            nc.sync.dma_start(out=late[a][0 : P - 4 * a, :].bitcast(I32), in_=glast[4 * a : P, :].bitcast(I32))
+            nc.sync.dma_start(out=late[a][0:SHIFTED, :].bitcast(I32), in_=glast[4 * a : 4 * a + SHIFTED, :].bitcast(I32))
         nc.sync.dma_start(out=late[4][:].bitcast(I32), in_=glast[:].bitcast(I32))
-        g3_rest.append(held([P, LAST], U32, "g3_rest", tag="grouped_4_512"))
-        gather_words(g3_rest[0][:], 3, 0, LAST)
+        g3_rest.append(held([P, HELD], U32, "g3_rest", tag="grouped_4_512"))
+        gather_words(g3_rest[0][:], 3, 0, HELD)
         for blk in blocks:
             if blk[1] == 0:
-                for a in range(1 if blk[3] == LAST else 3, 4):
+                for a in range(1 if blk[3] == LAST else 4 if blk[3] >= HELD else 3, 4):
                     multiply(a, blk)
         gather_bytes(glate[:], 0, LAST)
+        gates = held([P, 2, T], F32, "gates", tag="packed")
+        nc.sync.dma_start(out=gates[:], in_=gate.rearrange("c p t -> p c t"))
         gwords[4] = held([P, LAST], U32, "gwords_4", tag="glast")
 
         for s0, s1 in ((1024, 1536), (640, 1024), (128, 640), (0, 128)):

@@ -121,7 +121,10 @@ def tile_moe_rag_lin_bias_kernel(tc, xT, w_words, w_scales, b, gate, offs, pos1,
                 if eng == "v":
                     nc.vector.tensor_copy(out=dst, in_=src)
                 else:
-                    nc.scalar.copy(out=dst, in_=src)
+                    nc.scalar.copy(
+                        out=dst.rearrange("p (c i) j -> p c j i", i=2),
+                        in_=raws[(a, c0)].rearrange("p j (c i) -> p c j i", i=2),
+                    )
 
         def quantize(a):
             for t0, t1 in quants:

@@ -23,8 +23,10 @@ N = 128
 A = 5
 LAST = 1024
 SHIFTED = 112
-HELD = 512
-WINDOW = 2048
+PARKED = 112
+THIRD = 256
+WIDE = 2048
+TAIL = 512
 
 
 def tile_moe_rag_lin_bias_kernel(tc, xT, w_words, w_scales, b, gate, offs, pos1, pos2, out):
@@ -39,156 +41,133 @@ def tile_moe_rag_lin_bias_kernel(tc, xT, w_words, w_scales, b, gate, offs, pos1,
         offs_t = held([P, S // 16], U16, "offs_t")
         pos1_t = held([P, T // 16], U16, "pos1_t")
         pos2_t = held([P, T // 16], U16, "pos2_t")
+        b_t = held([P, E], F32, "b_t")
 
-        loads = [
-            ((0, 512), (512, 768)),
-            ((0, 256), (256, 512), (512, 768)),
-            ((0, 256), (256, 512), (512, 768)),
-            ((0, 512), (512, 768)),
-            ((0, 512), (512, 768)),
-        ]
-        casts = [
-            ((0, 320, "v"), (320, 512, "s"), (512, 672, "v"), (672, 768, "s")),
-            ((0, 256, "s"), (256, 512, "s"), (512, 768, "s")),
-            ((0, 256, "s"), (256, 512, "s"), (512, 768, "s")),
-            ((0, 512, "s"), (512, 768, "s")),
-            ((0, 512, "s"), (512, 768, "s")),
-        ]
-        quants = ((0, 512), (512, 768))
-
+        thirds = (0, THIRD, 2 * THIRD)
         raws = {}
+        groups = {}
 
         def load(a):
             rows = xT[512 * a : 512 * (a + 1), :].rearrange("(p j) w -> p j w", j=4)
-            for t0, t1 in loads[a]:
-                raw = held([P, 4, t1 - t0], F32, "raw_%d_%d" % (a, t0))
-                nc.sync.dma_start(out=raw[:], in_=rows[:, :, t0:t1])
-                for c0, c1, eng in casts[a]:
-                    if t0 <= c0 < t1:
-                        raws[(a, c0)] = raw[:, :, c0 - t0 : c1 - t0]
+            for t0 in thirds:
+                raw = held([P, 4, THIRD], F32, "raw_%d_%d" % (a, t0), tag="raw_%d_%d" % (a % 3, t0))
+                nc.sync.dma_start(out=raw[:], in_=rows[:, :, t0 : t0 + THIRD])
+                raws[(a, t0)] = raw
 
         load(0)
         nc.sync.dma_start(offs_t[:], offs)
-        nc.sync.dma_start(pos1_t[:], pos1)
-        nc.sync.dma_start(pos2_t[:], pos2)
-        b_t = held([P, E], F32, "b_t")
-        nc.sync.dma_start(out=b_t[:], in_=b)
-        for a in range(1, A - 1):
-            load(a)
+        load(1)
+        load(2)
 
-        words = held([P, E * A * 2 * N], U8, "words")
         wplane = held([P, E * A * N], U8, "wplane")
-        packed = held([P, WINDOW], U8, "packed")
-        codes = held([P, (A - 1) * T + WINDOW], U32, "codes")
+        plane0 = held([P, T], U8, "plane0")
+        packed = held([P, T], U8, "packed")
+        joined = held([P, WIDE], U8, "joined")
+        codes = held([P, A * T + TAIL], U32, "codes")
+        nc.gpsimd.memset(wplane[:].bitcast(I32), 0)
         nc.vector.memset(codes[:, A * T :].bitcast(I32), 0)
+        nc.vector.memset(packed[:].bitcast(I32), 0)
+        nc.vector.memset(joined[:, T:].bitcast(I32), 0)
+        pieces = ((LAST, S), (0, LAST))
         moved = {}
-        for a in (1, 2, 3):
-            moved[a] = held([P, LAST], U8, "moved_%d" % a)
-        late = {}
-        for a in (1, 2, 3, 4):
-            late[a] = held([P, S - LAST], U8, "late_%d" % a)
-        for plane in (packed, wplane, moved[1], moved[2], moved[3], late[1], late[2], late[3]):
-            nc.vector.memset(plane[:].bitcast(I32), 0)
+        for a in (0, 2, 3, 4):
+            for s0, s1 in pieces:
+                moved[(a, s0)] = held([P, s1 - s0], U8, "moved_%d_%d" % (a, s0))
+                nc.vector.memset(moved[(a, s0)][:].bitcast(I32), 0)
 
         nc.sync.dma_start(
             out=wplane[0:16, :].bitcast(I32).rearrange("r (m c) -> r m c", m=E * A),
             in_=w_scales.bitcast(I32).rearrange("e a r c -> r (e a) c"),
         )
-        load(A - 1)
-        for q in range(1, 4):
-            nc.sync.dma_start(out=wplane[32 * q : 32 * q + 4, :].bitcast(I32), in_=wplane[4 * q : 4 * q + 4, :].bitcast(I32))
-        for e0, e1 in ((3, 6), (0, 3)):
-            nc.sync.dma_start(
-                out=words[:, 2 * N * A * e0 : 2 * N * A * e1].bitcast(I32).rearrange("p (m c) -> p m c", c=N // 2),
-                in_=w_words[e0:e1].bitcast(I32).rearrange("e a p c -> p (e a) c"),
-            )
+        nc.sync.dma_start(out=b_t[:], in_=b)
+        nc.sync.dma_start(pos1_t[:], pos1)
+        nc.sync.dma_start(pos2_t[:], pos2)
 
-        gwords = {}
-        for a in range(3):
-            gwords[a] = held([P, S], U32, "gwords_%d" % a)
-        gearly = held([P, S], U8, "gearly")
-        glate = held([P, LAST], U8, "glate")
-
-        groups = {}
+        def quants(a):
+            return ((0, 256), (256, 512), (512, 768)) if a == 0 else ((0, 512), (512, 768))
 
         def cast(a):
-            for t0, t1 in quants:
+            for t0, t1 in quants(a):
                 groups[(a, t0)] = held([P, t1 - t0, 4], BF16, "grouped_%d_%d" % (a, t0))
-            for c0, c1, eng in casts[a]:
-                t0 = 0 if c0 < 512 else 512
-                dst = groups[(a, t0)][:, c0 - t0 : c1 - t0, :]
-                src = raws[(a, c0)].rearrange("p j w -> p w j")
-                if eng == "v":
-                    nc.vector.tensor_copy(out=dst, in_=src)
-                else:
-                    nc.scalar.copy(
-                        out=dst.rearrange("p (c i) j -> p c j i", i=2),
-                        in_=raws[(a, c0)].rearrange("p j (c i) -> p c j i", i=2),
-                    )
+            for t0 in thirds:
+                g0 = max(q0 for q0, q1 in quants(a) if q0 <= t0)
+                share = 160 if a == 0 else 0
+                dst = groups[(a, g0)][:, t0 - g0 : t0 - g0 + THIRD, :]
+                src = raws[(a, t0)]
+                if share:
+                    nc.vector.tensor_copy(out=dst[:, 0:share, :], in_=src[:, :, 0:share].rearrange("p j w -> p w j"))
+                nc.scalar.copy(
+                    out=dst[:, share:, :].rearrange("p (c i) j -> p c j i", i=2),
+                    in_=src[:, :, share:].rearrange("p j (c i) -> p c j i", i=2),
+                )
 
         def quantize(a):
-            for t0, t1 in quants:
+            for t0, t1 in quants(a):
                 nc.vector.quantize_mx(
                     out=codes[:, (A - 1 - a) * T + t0 : (A - 1 - a) * T + t1].bitcast(FP8X4),
-                    scales=packed[4 * (a % 4) : P, t0:t1],
+                    scales=plane0[:, t0:t1] if a == 0 else packed[4 * (a - 1) : P, t0:t1],
                     in_=groups[(a, t0)][:].rearrange("p w j -> p (w j)"),
                 )
 
         def gather(dst, src, s0, s1):
             nc.vector.tensor_copy(dst, src.indirect(offs_t[:, s0 // 16 : s1 // 16]))
 
+        def window(n):
+            return T if n <= 512 else 1024 if n <= 768 else WIDE
+
         def gather_words(dst, a, s0, s1):
             first = (A - 1 - a) * T
-            gather(dst, codes[:, first : first + (WINDOW if s1 - s0 > 512 else T)], s0, s1)
+            gather(dst, codes[:, first : first + window(s1 - s0)], s0, s1)
 
-        def gather_bytes(dst, s0, s1):
-            gather(dst, packed[:, 0 : (WINDOW if s1 - s0 > 512 else T)], s0, s1)
+        gwords = {}
+        for a in range(3):
+            gwords[a] = held([P, S], U32, "gwords_%d" % a)
+        g3_early = held([P, S - LAST], U32, "g3_early")
+        gbytes = held([P, S], U8, "gbytes")
+        late = []
 
         def slot_words(a, s0, sn):
             if a == 3:
-                return g3_last[:, s0 - HELD : s0 - HELD + sn] if s0 >= HELD else g3_rest[0][:, s0 : s0 + sn]
-            if a == 4 and s0 >= LAST:
-                return g4_last[:, s0 - LAST : s0 - LAST + sn]
+                return g3_early[:, s0 - LAST : s0 - LAST + sn] if s0 >= LAST else late[0][:, s0 : s0 + sn]
+            if a == 4:
+                return late[0][:, LAST + s0 : LAST + s0 + sn]
             return gwords[a][:, s0 : s0 + sn]
 
         def slot_plane(a, s0, sn):
-            if a == 0:
-                return gearly[:, s0 : s0 + sn]
-            if s0 >= LAST:
-                return late[a][:, s0 - LAST : s0 - LAST + sn]
-            return moved[a][:, s0 : s0 + sn] if a < 4 else glate[:, s0 : s0 + sn]
-
-        g3_last = held([P, S - HELD], U32, "g3_last")
-        g4_last = held([P, S - LAST], U32, "g4_last")
-        g3_rest = []
+            if a == 1:
+                return gbytes[:, s0 : s0 + sn]
+            p0 = max(q0 for q0, q1 in pieces if q0 <= s0)
+            return moved[(a, p0)][:, s0 - p0 : s0 - p0 + sn]
 
         blocks = [
+            (7, 0, 5, 1024, 512),
             (6, 0, 4, 768, 128),
             (6, 128, 4, 896, 128),
             (5, 0, 4, 640, 128),
             (4, 0, 3, 512, 128),
-            (1, 0, 1, 128, 128),
-            (2, 0, 2, 256, 128),
             (3, 0, 3, 384, 128),
-            (7, 0, 5, 1024, 512),
+            (2, 0, 2, 256, 128),
+            (1, 0, 1, 128, 128),
             (0, 0, 0, 0, 128),
         ]
+        order = (1, 0, 2, 3, 4)
         banks = []
         for i in range(8):
             banks.append(psum.tile([P, 512], F32, name="bank_%d" % i))
         y = held([P, S], F32, "y")
+        weights = []
 
         def multiply(a, block):
             bank, col, e, s0, sn = block
             m = e * A + a
             nc.tensor.matmul_mx(
                 out=banks[bank][:, col : col + sn],
-                lhsT=words[:, 2 * N * m : 2 * N * (m + 1)].bitcast(FP4X4),
+                lhsT=weights[0][:, 2 * N * m : 2 * N * (m + 1)].bitcast(FP4X4),
                 lhsT_scale=wplane[:, N * m : N * (m + 1)],
                 rhs=slot_words(a, s0, sn).bitcast(FP8X4),
                 rhs_scale=slot_plane(a, s0, sn),
-                start=(a == 0),
-                stop=(a == A - 1),
+                start=(a == order[0]),
+                stop=(a == order[-1]),
             )
 
         def leave(bank, col, e, s0, sn):
@@ -198,49 +177,67 @@ def tile_moe_rag_lin_bias_kernel(tc, xT, w_words, w_scales, b, gate, offs, pos1,
                 nc.scalar.activation(out=y[:, s0 : s0 + sn], in_=banks[bank][:, col : col + sn], func=IDENTITY, bias=b_t[:, e : e + 1])
 
         cast(0)
-        cast(1)
+        load(3)
         quantize(0)
-        gather_bytes(gearly[:, LAST:S], LAST, S)
-        gather_words(gwords[0][:], 0, 0, S)
-        cast(2)
+        for q in range(4):
+            nc.sync.dma_start(
+                out=joined[PARKED + 4 * q : PARKED + 4 * q + 4, 0:T].bitcast(I32), in_=plane0[32 * q : 32 * q + 4, :].bitcast(I32)
+            )
+        gather_words(gwords[0][:, 0:T], 0, 0, T)
+        gather_words(gwords[0][:, T:S], 0, T, S)
+        cast(1)
+        load(4)
         quantize(1)
+        weights.append(held([P, E * A * 2 * N], U8, "words", tag="grouped_1_512"))
+        for e0, e1 in ((3, 6), (0, 3)):
+            nc.sync.dma_start(
+                out=weights[0][:, 2 * N * A * e0 : 2 * N * A * e1].bitcast(I32).rearrange("p (m c) -> p m c", c=N // 2),
+                in_=w_words[e0:e1].bitcast(I32).rearrange("e a p c -> p (e a) c"),
+            )
+        for q in range(1, 4):
+            nc.sync.dma_start(out=wplane[32 * q : 32 * q + 4, :].bitcast(I32), in_=wplane[4 * q : 4 * q + 4, :].bitcast(I32))
         gather_words(gwords[1][:], 1, 0, S)
-        cast(3)
+        cast(2)
         quantize(2)
-        gather_words(gwords[2][:], 2, 0, S)
-        cast(4)
-        quantize(3)
-        gather_bytes(gearly[:, 0:LAST], 0, LAST)
-        for a in (1, 2, 3):
-            nc.sync.dma_start(out=moved[a][0:SHIFTED, :].bitcast(I32), in_=gearly[4 * a : 4 * a + SHIFTED, 0:LAST].bitcast(I32))
-        gather_words(g3_last[:], 3, HELD, S)
-        for blk in blocks:
-            if blk[1] == 0:
-                for a in range(1 if blk[3] == LAST else 4 if blk[3] >= HELD else 3):
-                    multiply(a, blk)
-        quantize(4)
-        glast = held([P, S - LAST], U8, "glast")
-        gather_bytes(glast[:], LAST, S)
-        for a in (1, 2, 3):
-            nc.sync.dma_start(out=late[a][0:SHIFTED, :].bitcast(I32), in_=glast[4 * a : 4 * a + SHIFTED, :].bitcast(I32))
-        nc.sync.dma_start(out=late[4][:].bitcast(I32), in_=glast[:].bitcast(I32))
-        g3_rest.append(held([P, HELD], U32, "g3_rest", tag="grouped_4_512"))
-        gather_words(g3_rest[0][:], 3, 0, HELD)
-        for blk in blocks:
-            if blk[1] == 0:
-                for a in range(1 if blk[3] == LAST else 4 if blk[3] >= HELD else 3, 4):
-                    multiply(a, blk)
-        gather_bytes(glate[:], 0, LAST)
-        gates = held([P, 2, T], F32, "gates", tag="packed")
+        gates = held([P, 2, T], F32, "gates", tag="grouped_2_512")
         nc.sync.dma_start(out=gates[:], in_=gate.rearrange("c p t -> p c t"))
-        gwords[4] = held([P, LAST], U32, "gwords_4", tag="glast")
+        gather_words(gwords[2][:], 2, 0, S)
+        cast(3)
+        quantize(3)
+        gather_words(g3_early[:], 3, LAST, S)
+        cast(4)
+        quantize(4)
+        nc.vector.tensor_copy(out=joined[0:PARKED, 0:T].bitcast(I32), in_=packed[0:PARKED, :].bitcast(I32))
+        for s0, s1 in pieces:
+            gather(gbytes[:, s0:s1], joined[:, 0 : window(s1 - s0)], s0, s1)
+            for q in range(4):
+                nc.sync.dma_start(
+                    out=moved[(0, s0)][32 * q : 32 * q + 4, :].bitcast(I32),
+                    in_=gbytes[PARKED + 4 * q : PARKED + 4 * q + 4, s0:s1].bitcast(I32),
+                )
+            for a in (2, 3, 4):
+                k = 4 * (a - 1)
+                nc.sync.dma_start(out=moved[(a, s0)][0:SHIFTED, :].bitcast(I32), in_=gbytes[k : k + SHIFTED, s0:s1].bitcast(I32))
+        late.append(held([P, LAST + S], U32, "late", tag="joined"))
+        gather_words(late[0][:, 2 * LAST :], 4, LAST, S)
+        gather_words(late[0][:, 0:LAST], 3, 0, LAST)
+        for blk in blocks:
+            if blk[1] == 0:
+                multiply(1, blk)
+        for a in order[1:]:
+            multiply(a, blocks[0])
+        leave(*blocks[0])
+        for a in order[1:-1]:
+            for blk in blocks[1:]:
+                if blk[1] == 0:
+                    multiply(a, blk)
 
-        for s0, s1 in ((1024, 1536), (640, 1024), (128, 640), (0, 128)):
-            gather_words(g4_last[:] if s0 == LAST else gwords[4][:, s0:s1], 4, s0, s1)
+        for s0, s1 in ((640, 1024), (384, 640), (128, 384), (0, 128)):
+            gather_words(late[0][:, LAST + s0 : LAST + s1], 4, s0, s1)
             for blk in blocks:
                 if s0 <= blk[3] < s1:
                     if blk[1] > 0:
-                        for a in range(A - 1):
+                        for a in order[:-1]:
                             multiply(a, blk)
                     multiply(4, blk)
                     if blk[0] == 6:

@@ -41,17 +41,18 @@ def tile_moe_rag_lin_bias_kernel(tc, xT, w_words, w_scales, b, gate, offs, pos1,
         offs_t = held([P, S // 16], U16, "offs_t")
         pos1_t = held([P, T // 16], U16, "pos1_t")
         pos2_t = held([P, T // 16], U16, "pos2_t")
-        b_t = held([P, E], F32, "b_t")
 
-        thirds = (0, THIRD, 2 * THIRD)
+        thirds = ((0, 256), (256, 512), (512, 768))
+        uneven = ((0, 512), (512, 768))
+        loads = (uneven, thirds, uneven, uneven, thirds)
         raws = {}
         groups = {}
 
         def load(a):
             rows = xT[512 * a : 512 * (a + 1), :].rearrange("(p j) w -> p j w", j=4)
-            for t0 in thirds:
-                raw = held([P, 4, THIRD], F32, "raw_%d_%d" % (a, t0), tag="raw_%d_%d" % (a % 3, t0))
-                nc.sync.dma_start(out=raw[:], in_=rows[:, :, t0 : t0 + THIRD])
+            for t0, t1 in loads[a]:
+                raw = held([P, 4, t1 - t0], F32, "raw_%d_%d" % (a, t0))
+                nc.sync.dma_start(out=raw[:], in_=rows[:, :, t0:t1])
                 raws[(a, t0)] = raw
 
         load(0)
@@ -79,20 +80,21 @@ def tile_moe_rag_lin_bias_kernel(tc, xT, w_words, w_scales, b, gate, offs, pos1,
             out=wplane[0:16, :].bitcast(I32).rearrange("r (m c) -> r m c", m=E * A),
             in_=w_scales.bitcast(I32).rearrange("e a r c -> r (e a) c"),
         )
-        nc.sync.dma_start(out=b_t[:], in_=b)
+        load(3)
+        load(4)
         nc.sync.dma_start(pos1_t[:], pos1)
         nc.sync.dma_start(pos2_t[:], pos2)
 
         def quants(a):
-            return ((0, 256), (256, 512), (512, 768)) if a == 0 else ((0, 512), (512, 768))
+            return uneven
 
         def cast(a):
             for t0, t1 in quants(a):
                 groups[(a, t0)] = held([P, t1 - t0, 4], BF16, "grouped_%d_%d" % (a, t0))
-            for t0 in thirds:
+            for t0, t1 in loads[a]:
                 g0 = max(q0 for q0, q1 in quants(a) if q0 <= t0)
-                share = 160 if a == 0 else 0
-                dst = groups[(a, g0)][:, t0 - g0 : t0 - g0 + THIRD, :]
+                share = (t1 - t0) * 5 // 8 if a == 0 else 0
+                dst = groups[(a, g0)][:, t0 - g0 : t1 - g0, :]
                 src = raws[(a, t0)]
                 if share:
                     nc.vector.tensor_copy(out=dst[:, 0:share, :], in_=src[:, :, 0:share].rearrange("p j w -> p w j"))
@@ -123,7 +125,9 @@ def tile_moe_rag_lin_bias_kernel(tc, xT, w_words, w_scales, b, gate, offs, pos1,
         for a in range(3):
             gwords[a] = held([P, S], U32, "gwords_%d" % a)
         g3_early = held([P, S - LAST], U32, "g3_early")
-        gbytes = held([P, S], U8, "gbytes")
+        gbytes = {}
+        for s0, s1 in pieces:
+            gbytes[s0] = held([P, s1 - s0], U8, "gbytes_%d" % s0)
         late = []
 
         def slot_words(a, s0, sn):
@@ -134,10 +138,8 @@ def tile_moe_rag_lin_bias_kernel(tc, xT, w_words, w_scales, b, gate, offs, pos1,
             return gwords[a][:, s0 : s0 + sn]
 
         def slot_plane(a, s0, sn):
-            if a == 1:
-                return gbytes[:, s0 : s0 + sn]
             p0 = max(q0 for q0, q1 in pieces if q0 <= s0)
-            return moved[(a, p0)][:, s0 - p0 : s0 - p0 + sn]
+            return (gbytes[p0] if a == 1 else moved[(a, p0)])[:, s0 - p0 : s0 - p0 + sn]
 
         blocks = [
             (7, 0, 5, 1024, 512),
@@ -155,14 +157,21 @@ def tile_moe_rag_lin_bias_kernel(tc, xT, w_words, w_scales, b, gate, offs, pos1,
         for i in range(8):
             banks.append(psum.tile([P, 512], F32, name="bank_%d" % i))
         y = held([P, S], F32, "y")
-        weights = []
+        weights = {}
+
+        def load_weights(e0, tag):
+            weights[e0] = held([P, 3 * A * 2 * N], U8, "words_%d" % e0, tag=tag)
+            nc.sync.dma_start(
+                out=weights[e0][:].bitcast(I32).rearrange("p (m c) -> p m c", c=N // 2),
+                in_=w_words[e0 : e0 + 3].bitcast(I32).rearrange("e a p c -> p (e a) c"),
+            )
 
         def multiply(a, block):
             bank, col, e, s0, sn = block
             m = e * A + a
             nc.tensor.matmul_mx(
                 out=banks[bank][:, col : col + sn],
-                lhsT=weights[0][:, 2 * N * m : 2 * N * (m + 1)].bitcast(FP4X4),
+                lhsT=weights[e - e % 3][:, 2 * N * (m % (3 * A)) : 2 * N * (m % (3 * A) + 1)].bitcast(FP4X4),
                 lhsT_scale=wplane[:, N * m : N * (m + 1)],
                 rhs=slot_words(a, s0, sn).bitcast(FP8X4),
                 rhs_scale=slot_plane(a, s0, sn),
@@ -177,53 +186,49 @@ def tile_moe_rag_lin_bias_kernel(tc, xT, w_words, w_scales, b, gate, offs, pos1,
                 nc.scalar.activation(out=y[:, s0 : s0 + sn], in_=banks[bank][:, col : col + sn], func=IDENTITY, bias=b_t[:, e : e + 1])
 
         cast(0)
-        load(3)
         quantize(0)
         for q in range(4):
             nc.sync.dma_start(
                 out=joined[PARKED + 4 * q : PARKED + 4 * q + 4, 0:T].bitcast(I32), in_=plane0[32 * q : 32 * q + 4, :].bitcast(I32)
             )
+        load_weights(3, "grouped_0_512")
         gather_words(gwords[0][:, 0:T], 0, 0, T)
         gather_words(gwords[0][:, T:S], 0, T, S)
         cast(1)
-        load(4)
         quantize(1)
-        weights.append(held([P, E * A * 2 * N], U8, "words", tag="grouped_1_512"))
-        for e0, e1 in ((3, 6), (0, 3)):
-            nc.sync.dma_start(
-                out=weights[0][:, 2 * N * A * e0 : 2 * N * A * e1].bitcast(I32).rearrange("p (m c) -> p m c", c=N // 2),
-                in_=w_words[e0:e1].bitcast(I32).rearrange("e a p c -> p (e a) c"),
-            )
         for q in range(1, 4):
             nc.sync.dma_start(out=wplane[32 * q : 32 * q + 4, :].bitcast(I32), in_=wplane[4 * q : 4 * q + 4, :].bitcast(I32))
         gather_words(gwords[1][:], 1, 0, S)
         cast(2)
         quantize(2)
-        gates = held([P, 2, T], F32, "gates", tag="grouped_2_512")
-        nc.sync.dma_start(out=gates[:], in_=gate.rearrange("c p t -> p c t"))
+        load_weights(0, "grouped_2_512")
         gather_words(gwords[2][:], 2, 0, S)
         cast(3)
         quantize(3)
+        b_t = held([P, E], F32, "b_t", tag="grouped_3_512")
+        nc.sync.dma_start(out=b_t[:], in_=b)
         gather_words(g3_early[:], 3, LAST, S)
         cast(4)
         quantize(4)
         nc.vector.tensor_copy(out=joined[0:PARKED, 0:T].bitcast(I32), in_=packed[0:PARKED, :].bitcast(I32))
         for s0, s1 in pieces:
-            gather(gbytes[:, s0:s1], joined[:, 0 : window(s1 - s0)], s0, s1)
+            gather(gbytes[s0][:], joined[:, 0 : window(s1 - s0)], s0, s1)
             for q in range(4):
                 nc.sync.dma_start(
                     out=moved[(0, s0)][32 * q : 32 * q + 4, :].bitcast(I32),
-                    in_=gbytes[PARKED + 4 * q : PARKED + 4 * q + 4, s0:s1].bitcast(I32),
+                    in_=gbytes[s0][PARKED + 4 * q : PARKED + 4 * q + 4, :].bitcast(I32),
                 )
             for a in (2, 3, 4):
                 k = 4 * (a - 1)
-                nc.sync.dma_start(out=moved[(a, s0)][0:SHIFTED, :].bitcast(I32), in_=gbytes[k : k + SHIFTED, s0:s1].bitcast(I32))
+                nc.sync.dma_start(out=moved[(a, s0)][0:SHIFTED, :].bitcast(I32), in_=gbytes[s0][k : k + SHIFTED, :].bitcast(I32))
         late.append(held([P, LAST + S], U32, "late", tag="joined"))
         gather_words(late[0][:, 2 * LAST :], 4, LAST, S)
         gather_words(late[0][:, 0:LAST], 3, 0, LAST)
         for blk in blocks:
             if blk[1] == 0:
                 multiply(1, blk)
+        gates = held([P, 2, T], F32, "gates", tag="gbytes_%d" % LAST)
+        nc.sync.dma_start(out=gates[:], in_=gate.rearrange("c p t -> p c t"))
         for a in order[1:]:
             multiply(a, blocks[0])
         leave(*blocks[0])

@@ -24,7 +24,7 @@ A = 5
 LAST = 1024
 SHIFTED = 112
 PARKED = 112
-THIRD = 256
+HELD = 768
 WIDE = 2048
 TAIL = 512
 
@@ -42,9 +42,9 @@ def tile_moe_rag_lin_bias_kernel(tc, xT, w_words, w_scales, b, gate, offs, pos1,
         pos1_t = held([P, T // 16], U16, "pos1_t")
         pos2_t = held([P, T // 16], U16, "pos2_t")
 
-        thirds = ((0, 256), (256, 512), (512, 768))
         uneven = ((0, 512), (512, 768))
-        loads = (uneven, thirds, uneven, uneven, thirds)
+        whole = ((0, T),)
+        loads = (uneven, whole, whole, whole, whole)
         raws = {}
         groups = {}
 
@@ -63,24 +63,25 @@ def tile_moe_rag_lin_bias_kernel(tc, xT, w_words, w_scales, b, gate, offs, pos1,
         wplane = held([P, E * A * N], U8, "wplane")
         plane0 = held([P, T], U8, "plane0")
         packed = held([P, T], U8, "packed")
-        joined = held([P, WIDE], U8, "joined")
+        joined = held([P, 1024], U8, "joined")
         codes = held([P, A * T + TAIL], U32, "codes")
         nc.gpsimd.memset(wplane[:].bitcast(I32), 0)
         nc.vector.memset(codes[:, A * T :].bitcast(I32), 0)
         nc.vector.memset(packed[:].bitcast(I32), 0)
         nc.vector.memset(joined[:, T:].bitcast(I32), 0)
-        pieces = ((LAST, S), (0, LAST))
+        pieces = ((T, S), (0, T))
         moved = {}
         for a in (0, 2, 3, 4):
             for s0, s1 in pieces:
                 moved[(a, s0)] = held([P, s1 - s0], U8, "moved_%d_%d" % (a, s0))
                 nc.vector.memset(moved[(a, s0)][:].bitcast(I32), 0)
 
+        load(3)
+        wstage = held([16, E * A * N], U8, "wstage")
         nc.sync.dma_start(
-            out=wplane[0:16, :].bitcast(I32).rearrange("r (m c) -> r m c", m=E * A),
+            out=wstage[:].bitcast(I32).rearrange("r (m c) -> r m c", m=E * A),
             in_=w_scales.bitcast(I32).rearrange("e a r c -> r (e a) c"),
         )
-        load(3)
         load(4)
         nc.sync.dma_start(pos1_t[:], pos1)
         nc.sync.dma_start(pos2_t[:], pos2)
@@ -89,19 +90,25 @@ def tile_moe_rag_lin_bias_kernel(tc, xT, w_words, w_scales, b, gate, offs, pos1,
             return uneven
 
         def cast(a):
-            for t0, t1 in quants(a):
-                groups[(a, t0)] = held([P, t1 - t0, 4], BF16, "grouped_%d_%d" % (a, t0))
-            for t0, t1 in loads[a]:
-                g0 = max(q0 for q0, q1 in quants(a) if q0 <= t0)
-                share = (t1 - t0) * 5 // 8 if a == 0 else 0
-                dst = groups[(a, g0)][:, t0 - g0 : t1 - g0, :]
-                src = raws[(a, t0)]
-                if share:
-                    nc.vector.tensor_copy(out=dst[:, 0:share, :], in_=src[:, :, 0:share].rearrange("p j w -> p w j"))
-                nc.scalar.copy(
-                    out=dst[:, share:, :].rearrange("p (c i) j -> p c j i", i=2),
-                    in_=src[:, :, share:].rearrange("p j (c i) -> p c j i", i=2),
-                )
+            for t0, t1 in uneven:
+                dst = held([P, t1 - t0, 4], BF16, "grouped_%d_%d" % (a, t0))
+                groups[(a, t0)] = dst
+                for l0, l1 in loads[a]:
+                    c0, c1 = max(t0, l0), min(t1, l1)
+                    if c0 >= c1:
+                        continue
+                    share = (c1 - c0) * 5 // 8 if a == 0 else 256 if (a, t0) == (1, 512) else 0
+                    src = raws[(a, l0)]
+                    if share:
+                        nc.vector.tensor_copy(
+                            out=dst[:, c0 - t0 : c0 - t0 + share, :],
+                            in_=src[:, :, c0 - l0 : c0 - l0 + share].rearrange("p j w -> p w j"),
+                        )
+                    if c0 + share < c1:
+                        nc.scalar.copy(
+                            out=dst[:, c0 - t0 + share : c1 - t0, :].rearrange("p (c i) j -> p c j i", i=2),
+                            in_=src[:, :, c0 - l0 + share : c1 - l0].rearrange("p j (c i) -> p c j i", i=2),
+                        )
 
         def quantize(a):
             for t0, t1 in quants(a):
@@ -124,7 +131,7 @@ def tile_moe_rag_lin_bias_kernel(tc, xT, w_words, w_scales, b, gate, offs, pos1,
         gwords = {}
         for a in range(3):
             gwords[a] = held([P, S], U32, "gwords_%d" % a)
-        g3_early = held([P, S - LAST], U32, "g3_early")
+        g3_early = held([P, S - HELD], U32, "g3_early")
         gbytes = {}
         for s0, s1 in pieces:
             gbytes[s0] = held([P, s1 - s0], U8, "gbytes_%d" % s0)
@@ -132,9 +139,9 @@ def tile_moe_rag_lin_bias_kernel(tc, xT, w_words, w_scales, b, gate, offs, pos1,
 
         def slot_words(a, s0, sn):
             if a == 3:
-                return g3_early[:, s0 - LAST : s0 - LAST + sn] if s0 >= LAST else late[0][:, s0 : s0 + sn]
+                return g3_early[:, s0 - HELD : s0 - HELD + sn] if s0 >= HELD else late[0][:, s0 : s0 + sn]
             if a == 4:
-                return late[0][:, LAST + s0 : LAST + s0 + sn]
+                return late[0][:, HELD + s0 : HELD + s0 + sn]
             return gwords[a][:, s0 : s0 + sn]
 
         def slot_plane(a, s0, sn):
@@ -196,60 +203,57 @@ def tile_moe_rag_lin_bias_kernel(tc, xT, w_words, w_scales, b, gate, offs, pos1,
         gather_words(gwords[0][:, T:S], 0, T, S)
         cast(1)
         quantize(1)
-        for q in range(1, 4):
-            nc.sync.dma_start(out=wplane[32 * q : 32 * q + 4, :].bitcast(I32), in_=wplane[4 * q : 4 * q + 4, :].bitcast(I32))
         gather_words(gwords[1][:], 1, 0, S)
         cast(2)
         quantize(2)
-        load_weights(0, "grouped_2_512")
+        b_t = held([P, E], F32, "b_t", tag="grouped_2_0")
+        nc.sync.dma_start(out=b_t[:], in_=b)
+        for q in range(4):
+            nc.sync.dma_start(out=wplane[32 * q : 32 * q + 4, :].bitcast(I32), in_=wstage[4 * q : 4 * q + 4, :].bitcast(I32))
         gather_words(gwords[2][:], 2, 0, S)
         cast(3)
         quantize(3)
-        b_t = held([P, E], F32, "b_t", tag="grouped_3_512")
-        nc.sync.dma_start(out=b_t[:], in_=b)
-        gather_words(g3_early[:], 3, LAST, S)
+        load_weights(0, "grouped_3_0")
+        gather_words(g3_early[:], 3, HELD, S)
         cast(4)
         quantize(4)
         nc.vector.tensor_copy(out=joined[0:PARKED, 0:T].bitcast(I32), in_=packed[0:PARKED, :].bitcast(I32))
         for s0, s1 in pieces:
             gather(gbytes[s0][:], joined[:, 0 : window(s1 - s0)], s0, s1)
+            queue = nc.sync
             for q in range(4):
-                nc.sync.dma_start(
+                queue.dma_start(
                     out=moved[(0, s0)][32 * q : 32 * q + 4, :].bitcast(I32),
                     in_=gbytes[s0][PARKED + 4 * q : PARKED + 4 * q + 4, :].bitcast(I32),
                 )
             for a in (2, 3, 4):
                 k = 4 * (a - 1)
-                nc.sync.dma_start(out=moved[(a, s0)][0:SHIFTED, :].bitcast(I32), in_=gbytes[s0][k : k + SHIFTED, :].bitcast(I32))
-        late.append(held([P, LAST + S], U32, "late", tag="joined"))
-        gather_words(late[0][:, 2 * LAST :], 4, LAST, S)
-        gather_words(late[0][:, 0:LAST], 3, 0, LAST)
+                (nc.sync if a == 3 else nc.scalar).dma_start(out=moved[(a, s0)][0:SHIFTED, :].bitcast(I32), in_=gbytes[s0][k : k + SHIFTED, :].bitcast(I32))
+        late.append(held([P, HELD + S], U32, "late", tag="joined"))
+        gather_words(late[0][:, HELD + T :], 4, T, S)
+        gather_words(late[0][:, 0:HELD], 3, 0, HELD)
         for blk in blocks:
             if blk[1] == 0:
                 multiply(1, blk)
-        gates = held([P, 2, T], F32, "gates", tag="gbytes_%d" % LAST)
-        nc.sync.dma_start(out=gates[:], in_=gate.rearrange("c p t -> p c t"))
         for a in order[1:]:
-            multiply(a, blocks[0])
+            for blk in blocks[0:2]:
+                multiply(a, blk)
         leave(*blocks[0])
+        for a in order:
+            multiply(a, blocks[2])
+        leave(6, 0, 4, 768, 256)
+        gates = held([P, 2, T], F32, "gates", tag="gbytes_%d" % T)
+        for c in range(2):
+            nc.sync.dma_start(out=gates[:, c, :], in_=gate[c])
         for a in order[1:-1]:
-            for blk in blocks[1:]:
-                if blk[1] == 0:
-                    multiply(a, blk)
-
-        for s0, s1 in ((640, 1024), (384, 640), (128, 384), (0, 128)):
-            gather_words(late[0][:, LAST + s0 : LAST + s1], 4, s0, s1)
+            for blk in blocks[3:]:
+                multiply(a, blk)
+        for s0, s1 in ((384, 768), (128, 384), (0, 128)):
+            gather_words(late[0][:, HELD + s0 : HELD + s1], 4, s0, s1)
             for blk in blocks:
                 if s0 <= blk[3] < s1:
-                    if blk[1] > 0:
-                        for a in order[:-1]:
-                            multiply(a, blk)
                     multiply(4, blk)
-                    if blk[0] == 6:
-                        if blk[1] > 0:
-                            leave(6, 0, 4, 768, 256)
-                    else:
-                        leave(*blk)
+                    leave(*blk)
 
         terms = {}
 

@@ -24,7 +24,6 @@ A = 5
 LAST = 1024
 SHIFTED = 112
 PARKED = 112
-HELD = 768
 WIDE = 2048
 TAIL = 512
 
@@ -42,16 +41,17 @@ def tile_moe_rag_lin_bias_kernel(tc, xT, w_words, w_scales, b, gate, offs, pos1,
         pos1_t = held([P, T // 16], U16, "pos1_t")
         pos2_t = held([P, T // 16], U16, "pos2_t")
 
+        thirds = ((0, 256), (256, 512), (512, 768))
         uneven = ((0, 512), (512, 768))
         whole = ((0, T),)
-        loads = (uneven, whole, whole, whole, whole)
+        loads = (uneven, thirds, uneven, uneven, thirds)
         raws = {}
         groups = {}
 
         def load(a):
             rows = xT[512 * a : 512 * (a + 1), :].rearrange("(p j) w -> p j w", j=4)
             for t0, t1 in loads[a]:
-                raw = held([P, 4, t1 - t0], F32, "raw_%d_%d" % (a, t0))
+                raw = held([P, 4, t1 - t0], F32, "raw_%d_%d" % (a, t0), tag="raw_%d_%d" % (1 if a == 4 else a, t0))
                 nc.sync.dma_start(out=raw[:], in_=rows[:, :, t0:t1])
                 raws[(a, t0)] = raw
 
@@ -63,26 +63,18 @@ def tile_moe_rag_lin_bias_kernel(tc, xT, w_words, w_scales, b, gate, offs, pos1,
         wplane = held([P, E * A * N], U8, "wplane")
         plane0 = held([P, T], U8, "plane0")
         packed = held([P, T], U8, "packed")
-        joined = held([P, 1024], U8, "joined")
+        joined = held([P, 1536], U8, "joined")
         codes = held([P, A * T + TAIL], U32, "codes")
         nc.gpsimd.memset(wplane[:].bitcast(I32), 0)
         nc.vector.memset(codes[:, A * T :].bitcast(I32), 0)
         nc.vector.memset(packed[:].bitcast(I32), 0)
         nc.vector.memset(joined[:, T:].bitcast(I32), 0)
-        pieces = ((T, S), (0, T))
         moved = {}
-        for a in (0, 2, 3, 4):
-            for s0, s1 in pieces:
-                moved[(a, s0)] = held([P, s1 - s0], U8, "moved_%d_%d" % (a, s0))
-                nc.vector.memset(moved[(a, s0)][:].bitcast(I32), 0)
+        for a, s0, s1 in ((3, LAST, S), (4, LAST, S), (0, 0, S), (2, 0, S), (3, 0, LAST), (4, 0, LAST)):
+            moved[(a, s0)] = held([P, s1 - s0], U8, "moved_%d_%d" % (a, s0))
+            nc.vector.memset(moved[(a, s0)][:].bitcast(I32), 0)
 
         load(3)
-        wstage = held([16, E * A * N], U8, "wstage")
-        nc.sync.dma_start(
-            out=wstage[:].bitcast(I32).rearrange("r (m c) -> r m c", m=E * A),
-            in_=w_scales.bitcast(I32).rearrange("e a r c -> r (e a) c"),
-        )
-        load(4)
         nc.sync.dma_start(pos1_t[:], pos1)
         nc.sync.dma_start(pos2_t[:], pos2)
 
@@ -97,7 +89,7 @@ def tile_moe_rag_lin_bias_kernel(tc, xT, w_words, w_scales, b, gate, offs, pos1,
                     c0, c1 = max(t0, l0), min(t1, l1)
                     if c0 >= c1:
                         continue
-                    share = (c1 - c0) * 5 // 8 if a == 0 else 256 if (a, t0) == (1, 512) else 0
+                    share = (c1 - c0) * 5 // 8 if a == 0 or (a, t0) == (4, 512) else 0
                     src = raws[(a, l0)]
                     if share:
                         nc.vector.tensor_copy(
@@ -131,35 +123,31 @@ def tile_moe_rag_lin_bias_kernel(tc, xT, w_words, w_scales, b, gate, offs, pos1,
         gwords = {}
         for a in range(3):
             gwords[a] = held([P, S], U32, "gwords_%d" % a)
-        g3_early = held([P, S - HELD], U32, "g3_early")
-        gbytes = {}
-        for s0, s1 in pieces:
-            gbytes[s0] = held([P, s1 - s0], U8, "gbytes_%d" % s0)
+        gbytes = held([P, S], U8, "gbytes")
         late = []
 
         def slot_words(a, s0, sn):
-            if a == 3:
-                return g3_early[:, s0 - HELD : s0 - HELD + sn] if s0 >= HELD else late[0][:, s0 : s0 + sn]
-            if a == 4:
-                return late[0][:, HELD + s0 : HELD + s0 + sn]
+            if a >= 3:
+                return late[0][:, (a - 3) * S + s0 : (a - 3) * S + s0 + sn]
             return gwords[a][:, s0 : s0 + sn]
 
         def slot_plane(a, s0, sn):
-            p0 = max(q0 for q0, q1 in pieces if q0 <= s0)
-            return (gbytes[p0] if a == 1 else moved[(a, p0)])[:, s0 - p0 : s0 - p0 + sn]
+            if a == 1:
+                return gbytes[:, s0 : s0 + sn]
+            p0 = LAST if a > 2 and s0 >= LAST else 0
+            return moved[(a, p0)][:, s0 - p0 : s0 - p0 + sn]
 
-        blocks = [
-            (7, 0, 5, 1024, 512),
-            (6, 0, 4, 768, 128),
-            (6, 128, 4, 896, 128),
-            (5, 0, 4, 640, 128),
-            (4, 0, 3, 512, 128),
-            (3, 0, 3, 384, 128),
-            (2, 0, 2, 256, 128),
-            (1, 0, 1, 128, 128),
-            (0, 0, 0, 0, 128),
+        first = (7, 5, 1024, 512)
+        second = (7, 4, 896, 128)
+        lower = [
+            (6, 4, 768, 128),
+            (5, 4, 640, 128),
+            (4, 3, 512, 128),
+            (3, 3, 384, 128),
+            (2, 2, 256, 128),
+            (1, 1, 128, 128),
+            (0, 0, 0, 128),
         ]
-        order = (1, 0, 2, 3, 4)
         banks = []
         for i in range(8):
             banks.append(psum.tile([P, 512], F32, name="bank_%d" % i))
@@ -174,23 +162,23 @@ def tile_moe_rag_lin_bias_kernel(tc, xT, w_words, w_scales, b, gate, offs, pos1,
             )
 
         def multiply(a, block):
-            bank, col, e, s0, sn = block
+            bank, e, s0, sn = block
             m = e * A + a
             nc.tensor.matmul_mx(
-                out=banks[bank][:, col : col + sn],
+                out=banks[bank][:, 0:sn],
                 lhsT=weights[e - e % 3][:, 2 * N * (m % (3 * A)) : 2 * N * (m % (3 * A) + 1)].bitcast(FP4X4),
                 lhsT_scale=wplane[:, N * m : N * (m + 1)],
                 rhs=slot_words(a, s0, sn).bitcast(FP8X4),
                 rhs_scale=slot_plane(a, s0, sn),
-                start=(a == order[0]),
-                stop=(a == order[-1]),
+                start=(a == 1),
+                stop=(a == (0 if s0 >= LAST else 4)),
             )
 
-        def leave(bank, col, e, s0, sn):
+        def leave(bank, e, s0, sn):
             if s0 == 0:
-                nc.vector.tensor_scalar_add(out=y[:, s0 : s0 + sn], in0=banks[bank][:, col : col + sn], scalar1=b_t[:, e : e + 1])
+                nc.vector.tensor_scalar_add(out=y[:, s0 : s0 + sn], in0=banks[bank][:, 0:sn], scalar1=b_t[:, e : e + 1])
             else:
-                nc.scalar.activation(out=y[:, s0 : s0 + sn], in_=banks[bank][:, col : col + sn], func=IDENTITY, bias=b_t[:, e : e + 1])
+                nc.scalar.activation(out=y[:, s0 : s0 + sn], in_=banks[bank][:, 0:sn], func=IDENTITY, bias=b_t[:, e : e + 1])
 
         cast(0)
         quantize(0)
@@ -198,11 +186,17 @@ def tile_moe_rag_lin_bias_kernel(tc, xT, w_words, w_scales, b, gate, offs, pos1,
             nc.sync.dma_start(
                 out=joined[PARKED + 4 * q : PARKED + 4 * q + 4, 0:T].bitcast(I32), in_=plane0[32 * q : 32 * q + 4, :].bitcast(I32)
             )
-        load_weights(3, "grouped_0_512")
         gather_words(gwords[0][:, 0:T], 0, 0, T)
         gather_words(gwords[0][:, T:S], 0, T, S)
         cast(1)
+        load(4)
         quantize(1)
+        wstage = held([16, E * A * N], U8, "wstage", tag="grouped_1_0")
+        nc.sync.dma_start(
+            out=wstage[:].bitcast(I32).rearrange("r (m c) -> r m c", m=E * A),
+            in_=w_scales.bitcast(I32).rearrange("e a r c -> r (e a) c"),
+        )
+        load_weights(3, "grouped_1_512")
         gather_words(gwords[1][:], 1, 0, S)
         cast(2)
         quantize(2)
@@ -213,45 +207,50 @@ def tile_moe_rag_lin_bias_kernel(tc, xT, w_words, w_scales, b, gate, offs, pos1,
         gather_words(gwords[2][:], 2, 0, S)
         cast(3)
         quantize(3)
-        load_weights(0, "grouped_3_0")
-        gather_words(g3_early[:], 3, HELD, S)
         cast(4)
         quantize(4)
+        load_weights(0, "grouped_4_512")
         nc.vector.tensor_copy(out=joined[0:PARKED, 0:T].bitcast(I32), in_=packed[0:PARKED, :].bitcast(I32))
-        for s0, s1 in pieces:
-            gather(gbytes[s0][:], joined[:, 0 : window(s1 - s0)], s0, s1)
-            queue = nc.sync
-            for q in range(4):
-                queue.dma_start(
-                    out=moved[(0, s0)][32 * q : 32 * q + 4, :].bitcast(I32),
-                    in_=gbytes[s0][PARKED + 4 * q : PARKED + 4 * q + 4, :].bitcast(I32),
-                )
-            for a in (2, 3, 4):
-                k = 4 * (a - 1)
-                (nc.sync if a == 3 else nc.scalar).dma_start(out=moved[(a, s0)][0:SHIFTED, :].bitcast(I32), in_=gbytes[s0][k : k + SHIFTED, :].bitcast(I32))
-        late.append(held([P, HELD + S], U32, "late", tag="joined"))
-        gather_words(late[0][:, HELD + T :], 4, T, S)
-        gather_words(late[0][:, 0:HELD], 3, 0, HELD)
-        for blk in blocks:
-            if blk[1] == 0:
-                multiply(1, blk)
-        for a in order[1:]:
-            for blk in blocks[0:2]:
-                multiply(a, blk)
-        leave(*blocks[0])
-        for a in order:
-            multiply(a, blocks[2])
-        leave(6, 0, 4, 768, 256)
-        gates = held([P, 2, T], F32, "gates", tag="gbytes_%d" % T)
+
+        def shift(a, s0, s1):
+            k = 4 * (a - 1)
+            nc.sync.dma_start(out=moved[(a, s0)][0:SHIFTED, :].bitcast(I32), in_=gbytes[k : k + SHIFTED, s0:s1].bitcast(I32))
+
+        gather(gbytes[:, LAST:S], joined[:, 0:T], LAST, S)
+        shift(3, LAST, S)
+        shift(4, LAST, S)
+        gather(gbytes[:, 0:LAST], joined[:], 0, LAST)
+        shift(2, 0, S)
+        for q in range(4):
+            nc.sync.dma_start(
+                out=moved[(0, 0)][32 * q : 32 * q + 4, :].bitcast(I32), in_=gbytes[PARKED + 4 * q : PARKED + 4 * q + 4, :].bitcast(I32)
+            )
+        shift(3, 0, LAST)
+        shift(4, 0, LAST)
+        late.append(held([P, 2 * S], U32, "late", tag="joined"))
+        gather_words(late[0][:, LAST:S], 3, LAST, S)
+        gather_words(late[0][:, S + LAST :], 4, LAST, S)
+        gather_words(late[0][:, 0:LAST], 3, 0, LAST)
+        for blk in [first] + lower:
+            multiply(1, blk)
+        for a in (3, 4):
+            multiply(a, first)
+        gates = held([P, 2, T], F32, "gates", tag="moved_3_%d" % LAST)
         for c in range(2):
-            nc.sync.dma_start(out=gates[:, c, :], in_=gate[c])
-        for a in order[1:-1]:
-            for blk in blocks[3:]:
+            nc.sync.dma_start(out=gates[:, c, 0:512], in_=gate[c, :, 0:512])
+        nc.sync.dma_start(out=gates[:, :, 512:T], in_=gate[:, :, 512:T].rearrange("c p t -> p c t"))
+        for a in (2, 0):
+            for blk in [first] + lower:
                 multiply(a, blk)
-        for s0, s1 in ((384, 768), (128, 384), (0, 128)):
-            gather_words(late[0][:, HELD + s0 : HELD + s1], 4, s0, s1)
-            for blk in blocks:
-                if s0 <= blk[3] < s1:
+        leave(*first)
+        for blk in lower:
+            multiply(3, blk)
+        for a in (1, 2, 0, 3):
+            multiply(a, second)
+        for s0, s1 in ((640, 1024), (384, 640), (128, 384), (0, 128)):
+            gather_words(late[0][:, S + s0 : S + s1], 4, s0, s1)
+            for blk in lower + [second]:
+                if s0 <= blk[2] < s1:
                     multiply(4, blk)
                     leave(*blk)
 

@@ -41,17 +41,16 @@ def tile_moe_rag_lin_bias_kernel(tc, xT, w_words, w_scales, b, gate, offs, pos1,
         pos1_t = held([P, T // 16], U16, "pos1_t")
         pos2_t = held([P, T // 16], U16, "pos2_t")
 
-        thirds = ((0, 256), (256, 512), (512, 768))
         uneven = ((0, 512), (512, 768))
         whole = ((0, T),)
-        loads = (uneven, thirds, uneven, uneven, thirds)
+        loads = (uneven, whole, whole, whole, whole)
         raws = {}
         groups = {}
 
         def load(a):
             rows = xT[512 * a : 512 * (a + 1), :].rearrange("(p j) w -> p j w", j=4)
             for t0, t1 in loads[a]:
-                raw = held([P, 4, t1 - t0], F32, "raw_%d_%d" % (a, t0), tag="raw_%d_%d" % (1 if a == 4 else a, t0))
+                raw = held([P, 4, t1 - t0], F32, "raw_%d_%d" % (a, t0))
                 nc.sync.dma_start(out=raw[:], in_=rows[:, :, t0:t1])
                 raws[(a, t0)] = raw
 
@@ -75,6 +74,12 @@ def tile_moe_rag_lin_bias_kernel(tc, xT, w_words, w_scales, b, gate, offs, pos1,
             nc.vector.memset(moved[(a, s0)][:].bitcast(I32), 0)
 
         load(3)
+        load(4)
+        wstage = held([16, E * A * N], U8, "wstage")
+        nc.sync.dma_start(
+            out=wstage[:].bitcast(I32).rearrange("r (m c) -> r m c", m=E * A),
+            in_=w_scales.bitcast(I32).rearrange("e a r c -> r (e a) c"),
+        )
         nc.sync.dma_start(pos1_t[:], pos1)
         nc.sync.dma_start(pos2_t[:], pos2)
 
@@ -89,7 +94,7 @@ def tile_moe_rag_lin_bias_kernel(tc, xT, w_words, w_scales, b, gate, offs, pos1,
                     c0, c1 = max(t0, l0), min(t1, l1)
                     if c0 >= c1:
                         continue
-                    share = (c1 - c0) * 5 // 8 if a == 0 or (a, t0) == (4, 512) else 0
+                    share = (c1 - c0) * 5 // 8 if a == 0 or (a, t0) == (4, 512) else c1 - c0 if (a, t0) == (1, 512) else 0
                     src = raws[(a, l0)]
                     if share:
                         nc.vector.tensor_copy(
@@ -171,11 +176,11 @@ def tile_moe_rag_lin_bias_kernel(tc, xT, w_words, w_scales, b, gate, offs, pos1,
                 rhs=slot_words(a, s0, sn).bitcast(FP8X4),
                 rhs_scale=slot_plane(a, s0, sn),
                 start=(a == 1),
-                stop=(a == (0 if s0 >= LAST else 4)),
+                stop=(a == (2 if s0 >= LAST else 4)),
             )
 
         def leave(bank, e, s0, sn):
-            if s0 == 0:
+            if s0 < 384:
                 nc.vector.tensor_scalar_add(out=y[:, s0 : s0 + sn], in0=banks[bank][:, 0:sn], scalar1=b_t[:, e : e + 1])
             else:
                 nc.scalar.activation(out=y[:, s0 : s0 + sn], in_=banks[bank][:, 0:sn], func=IDENTITY, bias=b_t[:, e : e + 1])
@@ -189,13 +194,7 @@ def tile_moe_rag_lin_bias_kernel(tc, xT, w_words, w_scales, b, gate, offs, pos1,
         gather_words(gwords[0][:, 0:T], 0, 0, T)
         gather_words(gwords[0][:, T:S], 0, T, S)
         cast(1)
-        load(4)
         quantize(1)
-        wstage = held([16, E * A * N], U8, "wstage", tag="grouped_1_0")
-        nc.sync.dma_start(
-            out=wstage[:].bitcast(I32).rearrange("r (m c) -> r m c", m=E * A),
-            in_=w_scales.bitcast(I32).rearrange("e a r c -> r (e a) c"),
-        )
         load_weights(3, "grouped_1_512")
         gather_words(gwords[1][:], 1, 0, S)
         cast(2)
@@ -209,7 +208,7 @@ def tile_moe_rag_lin_bias_kernel(tc, xT, w_words, w_scales, b, gate, offs, pos1,
         quantize(3)
         cast(4)
         quantize(4)
-        load_weights(0, "grouped_4_512")
+        load_weights(0, "grouped_4_0")
         nc.vector.tensor_copy(out=joined[0:PARKED, 0:T].bitcast(I32), in_=packed[0:PARKED, :].bitcast(I32))
 
         def shift(a, s0, s1):
@@ -220,11 +219,11 @@ def tile_moe_rag_lin_bias_kernel(tc, xT, w_words, w_scales, b, gate, offs, pos1,
         shift(3, LAST, S)
         shift(4, LAST, S)
         gather(gbytes[:, 0:LAST], joined[:], 0, LAST)
-        shift(2, 0, S)
         for q in range(4):
             nc.sync.dma_start(
                 out=moved[(0, 0)][32 * q : 32 * q + 4, :].bitcast(I32), in_=gbytes[PARKED + 4 * q : PARKED + 4 * q + 4, :].bitcast(I32)
             )
+        shift(2, 0, S)
         shift(3, 0, LAST)
         shift(4, 0, LAST)
         late.append(held([P, 2 * S], U32, "late", tag="joined"))
@@ -239,13 +238,13 @@ def tile_moe_rag_lin_bias_kernel(tc, xT, w_words, w_scales, b, gate, offs, pos1,
         for c in range(2):
             nc.sync.dma_start(out=gates[:, c, 0:512], in_=gate[c, :, 0:512])
         nc.sync.dma_start(out=gates[:, :, 512:T], in_=gate[:, :, 512:T].rearrange("c p t -> p c t"))
-        for a in (2, 0):
+        for a in (0, 2):
             for blk in [first] + lower:
                 multiply(a, blk)
         leave(*first)
         for blk in lower:
             multiply(3, blk)
-        for a in (1, 2, 0, 3):
+        for a in (1, 0, 2, 3):
             multiply(a, second)
         for s0, s1 in ((640, 1024), (384, 640), (128, 384), (0, 128)):
             gather_words(late[0][:, S + s0 : S + s1], 4, s0, s1)

@@ -13,6 +13,7 @@ U8 = mybir.dt.uint8
 FP8X4 = mybir.dt.float8_e4m3fn_x4
 FP4X4 = mybir.dt.float4_e2m1fn_x4
 MULT = mybir.AluOpType.mult
+COPY = mybir.ActivationFunctionType.Copy
 IDENTITY = mybir.ActivationFunctionType.Identity
 
 P = 128
@@ -21,11 +22,10 @@ S = 1536
 E = 6
 N = 128
 A = 5
-LAST = 1024
 SHIFTED = 112
 PARKED = 112
 WIDE = 2048
-TAIL = 512
+TAIL = 1280
 
 
 def tile_moe_rag_lin_bias_kernel(tc, xT, w_words, w_scales, b, gate, offs, pos1, pos2, out):
@@ -33,6 +33,7 @@ def tile_moe_rag_lin_bias_kernel(tc, xT, w_words, w_scales, b, gate, offs, pos1,
     with ExitStack() as ctx:
         pool = ctx.enter_context(tc.tile_pool(name="held", bufs=1))
         psum = ctx.enter_context(tc.psum_pool(name="psum", bufs=1))
+        shared = ctx.enter_context(tc.tile_pool(name="shared", bufs=1))
 
         def held(shape, dtype, name, tag=None):
             return pool.tile(shape, dtype, name=name, tag=tag or name, align_bytes=64)
@@ -62,16 +63,16 @@ def tile_moe_rag_lin_bias_kernel(tc, xT, w_words, w_scales, b, gate, offs, pos1,
         wplane = held([P, E * A * N], U8, "wplane")
         plane0 = held([P, T], U8, "plane0")
         packed = held([P, T], U8, "packed")
-        joined = held([P, 1536], U8, "joined")
+        joined = shared.tile([P, WIDE], U8, name="joined", offset=8 * S - WIDE // 2, align_bytes=64)
         codes = held([P, A * T + TAIL], U32, "codes")
         nc.gpsimd.memset(wplane[:].bitcast(I32), 0)
         nc.vector.memset(codes[:, A * T :].bitcast(I32), 0)
         nc.vector.memset(packed[:].bitcast(I32), 0)
         nc.vector.memset(joined[:, T:].bitcast(I32), 0)
         moved = {}
-        for a, s0, s1 in ((3, LAST, S), (4, LAST, S), (0, 0, S), (2, 0, S), (3, 0, LAST), (4, 0, LAST)):
-            moved[(a, s0)] = held([P, s1 - s0], U8, "moved_%d_%d" % (a, s0))
-            nc.vector.memset(moved[(a, s0)][:].bitcast(I32), 0)
+        for a in (0, 2, 3, 4):
+            moved[a] = held([P, S], U8, "moved_%d" % a)
+            nc.vector.memset(moved[a][:].bitcast(I32), 0)
 
         load(3)
         load(4)
@@ -139,31 +140,28 @@ def tile_moe_rag_lin_bias_kernel(tc, xT, w_words, w_scales, b, gate, offs, pos1,
         def slot_plane(a, s0, sn):
             if a == 1:
                 return gbytes[:, s0 : s0 + sn]
-            p0 = LAST if a > 2 and s0 >= LAST else 0
-            return moved[(a, p0)][:, s0 - p0 : s0 - p0 + sn]
+            return moved[a][:, s0 : s0 + sn]
 
-        first = (7, 5, 1024, 512)
-        second = (7, 4, 896, 128)
-        lower = [
-            (6, 4, 768, 128),
-            (5, 4, 640, 128),
-            (4, 3, 512, 128),
-            (3, 3, 384, 128),
+        blocks = [
+            (6, 5, 1024, 512),
+            (5, 4, 768, 256),
+            (4, 4, 640, 128),
+            (3, 3, 384, 256),
             (2, 2, 256, 128),
             (1, 1, 128, 128),
             (0, 0, 0, 128),
         ]
         banks = []
-        for i in range(8):
+        for i in range(7):
             banks.append(psum.tile([P, 512], F32, name="bank_%d" % i))
         y = held([P, S], F32, "y")
-        weights = {}
+        weights = []
 
-        def load_weights(e0, tag):
-            weights[e0] = held([P, 3 * A * 2 * N], U8, "words_%d" % e0, tag=tag)
+        def load_weights(tag):
+            weights.append(held([P, E * A * 2 * N], U8, "words", tag=tag))
             nc.sync.dma_start(
-                out=weights[e0][:].bitcast(I32).rearrange("p (m c) -> p m c", c=N // 2),
-                in_=w_words[e0 : e0 + 3].bitcast(I32).rearrange("e a p c -> p (e a) c"),
+                out=weights[0][:].bitcast(I32).rearrange("p (m c) -> p m c", c=N // 2),
+                in_=w_words.bitcast(I32).rearrange("e a p c -> p (e a) c"),
             )
 
         def multiply(a, block):
@@ -171,16 +169,16 @@ def tile_moe_rag_lin_bias_kernel(tc, xT, w_words, w_scales, b, gate, offs, pos1,
             m = e * A + a
             nc.tensor.matmul_mx(
                 out=banks[bank][:, 0:sn],
-                lhsT=weights[e - e % 3][:, 2 * N * (m % (3 * A)) : 2 * N * (m % (3 * A) + 1)].bitcast(FP4X4),
+                lhsT=weights[0][:, 2 * N * m : 2 * N * (m + 1)].bitcast(FP4X4),
                 lhsT_scale=wplane[:, N * m : N * (m + 1)],
                 rhs=slot_words(a, s0, sn).bitcast(FP8X4),
                 rhs_scale=slot_plane(a, s0, sn),
                 start=(a == 1),
-                stop=(a == (2 if s0 >= LAST else 4)),
+                stop=(a == 4),
             )
 
         def leave(bank, e, s0, sn):
-            if s0 < 384:
+            if s0 < 256:
                 nc.vector.tensor_scalar_add(out=y[:, s0 : s0 + sn], in0=banks[bank][:, 0:sn], scalar1=b_t[:, e : e + 1])
             else:
                 nc.scalar.activation(out=y[:, s0 : s0 + sn], in_=banks[bank][:, 0:sn], func=IDENTITY, bias=b_t[:, e : e + 1])
@@ -191,11 +189,10 @@ def tile_moe_rag_lin_bias_kernel(tc, xT, w_words, w_scales, b, gate, offs, pos1,
             nc.sync.dma_start(
                 out=joined[PARKED + 4 * q : PARKED + 4 * q + 4, 0:T].bitcast(I32), in_=plane0[32 * q : 32 * q + 4, :].bitcast(I32)
             )
-        gather_words(gwords[0][:, 0:T], 0, 0, T)
-        gather_words(gwords[0][:, T:S], 0, T, S)
+        load_weights("grouped_0_512")
+        gather_words(gwords[0][:], 0, 0, S)
         cast(1)
         quantize(1)
-        load_weights(3, "grouped_1_512")
         gather_words(gwords[1][:], 1, 0, S)
         cast(2)
         quantize(2)
@@ -208,67 +205,42 @@ def tile_moe_rag_lin_bias_kernel(tc, xT, w_words, w_scales, b, gate, offs, pos1,
         quantize(3)
         cast(4)
         quantize(4)
-        load_weights(0, "grouped_4_0")
         nc.vector.tensor_copy(out=joined[0:PARKED, 0:T].bitcast(I32), in_=packed[0:PARKED, :].bitcast(I32))
 
-        def shift(a, s0, s1):
-            k = 4 * (a - 1)
-            nc.sync.dma_start(out=moved[(a, s0)][0:SHIFTED, :].bitcast(I32), in_=gbytes[k : k + SHIFTED, s0:s1].bitcast(I32))
-
-        gather(gbytes[:, LAST:S], joined[:, 0:T], LAST, S)
-        shift(3, LAST, S)
-        shift(4, LAST, S)
-        gather(gbytes[:, 0:LAST], joined[:], 0, LAST)
+        gather(gbytes[:], joined[:], 0, S)
         for q in range(4):
             nc.sync.dma_start(
-                out=moved[(0, 0)][32 * q : 32 * q + 4, :].bitcast(I32), in_=gbytes[PARKED + 4 * q : PARKED + 4 * q + 4, :].bitcast(I32)
+                out=moved[0][32 * q : 32 * q + 4, :].bitcast(I32), in_=gbytes[PARKED + 4 * q : PARKED + 4 * q + 4, :].bitcast(I32)
             )
-        shift(2, 0, S)
-        shift(3, 0, LAST)
-        shift(4, 0, LAST)
-        late.append(held([P, 2 * S], U32, "late", tag="joined"))
-        gather_words(late[0][:, LAST:S], 3, LAST, S)
-        gather_words(late[0][:, S + LAST :], 4, LAST, S)
-        gather_words(late[0][:, 0:LAST], 3, 0, LAST)
-        for blk in [first] + lower:
-            multiply(1, blk)
-        for a in (3, 4):
-            multiply(a, first)
-        gates = held([P, 2, T], F32, "gates", tag="moved_3_%d" % LAST)
-        for c in range(2):
-            nc.sync.dma_start(out=gates[:, c, 0:512], in_=gate[c, :, 0:512])
-        nc.sync.dma_start(out=gates[:, :, 512:T], in_=gate[:, :, 512:T].rearrange("c p t -> p c t"))
-        for a in (0, 2):
-            for blk in [first] + lower:
-                multiply(a, blk)
-        leave(*first)
-        for blk in lower:
-            multiply(3, blk)
+        for a in (2, 3, 4):
+            k = 4 * (a - 1)
+            nc.sync.dma_start(out=moved[a][0:SHIFTED, :].bitcast(I32), in_=gbytes[k : k + SHIFTED, :].bitcast(I32))
+        gates = shared.tile([P, 2, T], F32, name="gates", offset=8 * S, align_bytes=64)
+        nc.sync.dma_start(out=gates[:], in_=gate.rearrange("c p t -> p c t"))
+        late.append(shared.tile([P, 2 * S], U32, name="late", offset=0, align_bytes=64))
+        gather_words(late[0][:, 0:S], 3, 0, S)
         for a in (1, 0, 2, 3):
-            multiply(a, second)
-        for s0, s1 in ((640, 1024), (384, 640), (128, 384), (0, 128)):
+            for blk in blocks:
+                multiply(a, blk)
+        for s0, s1 in ((1024, 1536), (640, 1024), (384, 640), (128, 384), (0, 128)):
             gather_words(late[0][:, S + s0 : S + s1], 4, s0, s1)
-            for blk in lower + [second]:
+            for blk in blocks:
                 if s0 <= blk[2] < s1:
                     multiply(4, blk)
                     leave(*blk)
 
-        terms = {}
-
-        def fetch(c, t0, t1):
-            pos = (pos1_t, pos2_t)[c]
-            term = held([P, t1 - t0], F32, "term_%d_%d" % (c, t0))
-            nc.vector.tensor_tensor(term[:], y[:].indirect(pos[:, t0 // 16 : t1 // 16]), gates[:, c, t0:t1], MULT)
-            terms[(c, t0)] = term
-
-        def finish(t0, t1):
+        halves = ((0, 512), (512, T))
+        first, picked, second = {}, {}, {}
+        for t0, t1 in halves:
+            picked[t0] = held([P, t1 - t0], F32, "picked_%d" % t0)
+            nc.scalar.activation(picked[t0][:], y[:].indirect(pos2_t[:, t0 // 16 : t1 // 16]), COPY)
+        for t0, t1 in halves:
+            first[t0] = held([P, t1 - t0], F32, "first_%d" % t0)
+            nc.vector.tensor_tensor(first[t0][:], y[:].indirect(pos1_t[:, t0 // 16 : t1 // 16]), gates[:, 0, t0:t1], MULT)
+        for t0, t1 in halves:
+            second[t0] = held([P, t1 - t0], F32, "second_%d" % t0)
+            nc.vector.tensor_tensor(second[t0][:], picked[t0][:], gates[:, 1, t0:t1], MULT)
+        for t0, t1 in halves:
             total = held([P, t1 - t0], F32, "total_%d" % t0)
-            nc.vector.tensor_add(out=total[:], in0=terms[(0, t0)][:], in1=terms[(1, t0)][:])
+            nc.vector.tensor_add(out=total[:], in0=first[t0][:], in1=second[t0][:])
             nc.sync.dma_start(out=out[:, t0:t1], in_=total[:])
-
-        fetch(0, 0, 512)
-        fetch(1, 0, 512)
-        fetch(0, 512, 768)
-        finish(0, 512)
-        fetch(1, 512, 768)
-        finish(512, 768)

@@ -84,32 +84,33 @@ def tile_moe_rag_lin_bias_kernel(tc, xT, w_words, w_scales, b, gate, offs, pos1,
         nc.sync.dma_start(pos1_t[:], pos1)
         nc.sync.dma_start(pos2_t[:], pos2)
 
-        def quants(a):
-            return uneven
+        shares = ((320, 160), (128, 256), (0, 192), (0, 0), (128, 256))
+
+        def interleave(copy, a, part, c0, c1):
+            t0 = uneven[part][0]
+            l0 = t0 if a == 0 else 0
+            copy(
+                out=groups[(a, t0)][:, c0 - t0 : c1 - t0, :].rearrange("p (c i) j -> p c j i", i=4),
+                in_=raws[(a, l0)][:, :, c0 - l0 : c1 - l0].rearrange("p j (c i) -> p c j i", i=4),
+            )
 
         def cast(a):
             for t0, t1 in uneven:
-                dst = held([P, t1 - t0, 4], BF16, "grouped_%d_%d" % (a, t0))
-                groups[(a, t0)] = dst
-                for l0, l1 in loads[a]:
-                    c0, c1 = max(t0, l0), min(t1, l1)
-                    if c0 >= c1:
-                        continue
-                    share = (c1 - c0) * 5 // 8 if a == 0 or (a, t0) == (4, 512) else c1 - c0 if (a, t0) == (1, 512) else 0
-                    src = raws[(a, l0)]
-                    if share:
-                        nc.vector.tensor_copy(
-                            out=dst[:, c0 - t0 : c0 - t0 + share, :],
-                            in_=src[:, :, c0 - l0 : c0 - l0 + share].rearrange("p j w -> p w j"),
-                        )
-                    if c0 + share < c1:
-                        nc.scalar.copy(
-                            out=dst[:, c0 - t0 + share : c1 - t0, :].rearrange("p (c i) j -> p c j i", i=2),
-                            in_=src[:, :, c0 - l0 + share : c1 - l0].rearrange("p j (c i) -> p c j i", i=2),
-                        )
+                groups[(a, t0)] = held([P, t1 - t0, 4], BF16, "grouped_%d_%d" % (a, t0))
+            for part, (t0, t1) in enumerate(uneven):
+                if t0 + shares[a][part] < t1:
+                    interleave(nc.scalar.copy, a, part, t0 + shares[a][part], t1)
+            for part in order(a):
+                t0 = uneven[part][0]
+                if shares[a][part]:
+                    interleave(nc.vector.tensor_copy, a, part, t0, t0 + shares[a][part])
+
+        def order(a):
+            return (1, 0) if shares[a][1] == 256 else (0, 1)
 
         def quantize(a):
-            for t0, t1 in quants(a):
+            for part in order(a):
+                t0, t1 = uneven[part]
                 nc.vector.quantize_mx(
                     out=codes[:, (A - 1 - a) * T + t0 : (A - 1 - a) * T + t1].bitcast(FP8X4),
                     scales=plane0[:, t0:t1] if a == 0 else packed[4 * (a - 1) : P, t0:t1],

@@ -22,6 +22,7 @@ S = 1536
 E = 6
 N = 128
 A = 5
+LAST = 1024
 SHIFTED = 112
 PARKED = 112
 WIDE = 2048
@@ -70,9 +71,9 @@ def tile_moe_rag_lin_bias_kernel(tc, xT, w_words, w_scales, b, gate, offs, pos1,
         nc.vector.memset(packed[:].bitcast(I32), 0)
         nc.vector.memset(joined[:, T:].bitcast(I32), 0)
         moved = {}
-        for a in (0, 2, 3, 4):
-            moved[a] = held([P, S], U8, "moved_%d" % a)
-            nc.vector.memset(moved[a][:].bitcast(I32), 0)
+        for a, s0, s1 in ((3, LAST, S), (4, LAST, S), (0, 0, S), (2, 0, S), (3, 0, LAST), (4, 0, LAST)):
+            moved[(a, s0)] = held([P, s1 - s0], U8, "moved_%d_%d" % (a, s0))
+            nc.vector.memset(moved[(a, s0)][:].bitcast(I32), 0)
 
         load(3)
         load(4)
@@ -84,7 +85,7 @@ def tile_moe_rag_lin_bias_kernel(tc, xT, w_words, w_scales, b, gate, offs, pos1,
         nc.sync.dma_start(pos1_t[:], pos1)
         nc.sync.dma_start(pos2_t[:], pos2)
 
-        shares = ((320, 160), (128, 256), (0, 192), (0, 0), (128, 256))
+        shares = ((320, 160), (0, 256), (0, 0), (0, 0), (64, 256))
 
         def interleave(copy, a, part, c0, c1):
             t0 = uneven[part][0]
@@ -141,7 +142,8 @@ def tile_moe_rag_lin_bias_kernel(tc, xT, w_words, w_scales, b, gate, offs, pos1,
         def slot_plane(a, s0, sn):
             if a == 1:
                 return gbytes[:, s0 : s0 + sn]
-            return moved[a][:, s0 : s0 + sn]
+            p0 = LAST if a > 2 and s0 >= LAST else 0
+            return moved[(a, p0)][:, s0 - p0 : s0 - p0 + sn]
 
         blocks = [
             (6, 5, 1024, 512),
@@ -175,7 +177,7 @@ def tile_moe_rag_lin_bias_kernel(tc, xT, w_words, w_scales, b, gate, offs, pos1,
                 rhs=slot_words(a, s0, sn).bitcast(FP8X4),
                 rhs_scale=slot_plane(a, s0, sn),
                 start=(a == 1),
-                stop=(a == 4),
+                stop=(a == (2 if s0 >= LAST else 4)),
             )
 
         def leave(bank, e, s0, sn):
@@ -208,22 +210,38 @@ def tile_moe_rag_lin_bias_kernel(tc, xT, w_words, w_scales, b, gate, offs, pos1,
         quantize(4)
         nc.vector.tensor_copy(out=joined[0:PARKED, 0:T].bitcast(I32), in_=packed[0:PARKED, :].bitcast(I32))
 
-        gather(gbytes[:], joined[:], 0, S)
+        def shift(a, s0, s1):
+            k = 4 * (a - 1)
+            nc.sync.dma_start(out=moved[(a, s0)][0:SHIFTED, :].bitcast(I32), in_=gbytes[k : k + SHIFTED, s0:s1].bitcast(I32))
+
+        gather(gbytes[:, LAST:S], joined[:, 0:T], LAST, S)
+        shift(3, LAST, S)
+        shift(4, LAST, S)
+        gather(gbytes[:, 0:LAST], joined[:], 0, LAST)
         for q in range(4):
             nc.sync.dma_start(
-                out=moved[0][32 * q : 32 * q + 4, :].bitcast(I32), in_=gbytes[PARKED + 4 * q : PARKED + 4 * q + 4, :].bitcast(I32)
+                out=moved[(0, 0)][32 * q : 32 * q + 4, :].bitcast(I32), in_=gbytes[PARKED + 4 * q : PARKED + 4 * q + 4, :].bitcast(I32)
             )
-        for a in (2, 3, 4):
-            k = 4 * (a - 1)
-            nc.sync.dma_start(out=moved[a][0:SHIFTED, :].bitcast(I32), in_=gbytes[k : k + SHIFTED, :].bitcast(I32))
+        shift(2, 0, S)
+        shift(3, 0, LAST)
+        shift(4, 0, LAST)
         gates = shared.tile([P, 2, T], F32, name="gates", offset=8 * S, align_bytes=64)
         nc.sync.dma_start(out=gates[:], in_=gate.rearrange("c p t -> p c t"))
         late.append(shared.tile([P, 2 * S], U32, name="late", offset=0, align_bytes=64))
-        gather_words(late[0][:, 0:S], 3, 0, S)
-        for a in (1, 0, 2, 3):
+        gather_words(late[0][:, LAST:S], 3, LAST, S)
+        gather_words(late[0][:, S + LAST :], 4, LAST, S)
+        gather_words(late[0][:, 0:LAST], 3, 0, LAST)
+        for blk in blocks:
+            multiply(1, blk)
+        for a in (3, 4):
+            multiply(a, blocks[0])
+        for a in (0, 2):
             for blk in blocks:
                 multiply(a, blk)
-        for s0, s1 in ((1024, 1536), (640, 1024), (384, 640), (128, 384), (0, 128)):
+        leave(*blocks[0])
+        for blk in blocks[1:]:
+            multiply(3, blk)
+        for s0, s1 in ((640, 1024), (384, 640), (128, 384), (0, 128)):
             gather_words(late[0][:, S + s0 : S + s1], 4, s0, s1)
             for blk in blocks:
                 if s0 <= blk[2] < s1:

@@ -91,8 +91,8 @@ def tile_moe_rag_lin_bias_kernel(tc, xT, w_words, w_scales, b, gate, offs, pos1,
             t0 = uneven[part][0]
             l0 = t0 if a == 0 else 0
             copy(
-                out=groups[(a, t0)][:, c0 - t0 : c1 - t0, :].rearrange("p (c i) j -> p c j i", i=4),
-                in_=raws[(a, l0)][:, :, c0 - l0 : c1 - l0].rearrange("p j (c i) -> p c j i", i=4),
+                out=groups[(a, t0)][:, c0 - t0 : c1 - t0, :].rearrange("p (c i) j -> p c j i", i=2),
+                in_=raws[(a, l0)][:, :, c0 - l0 : c1 - l0].rearrange("p j (c i) -> p c j i", i=2),
             )
 
         def cast(a):

@@ -158,13 +158,13 @@ def tile_moe_rag_lin_bias_kernel(tc, xT, w_words, w_scales, b, gate, offs, pos1,
         for i in range(7):
             banks.append(psum.tile([P, 512], F32, name="bank_%d" % i))
         y = held([P, S], F32, "y")
-        weights = []
+        weights = {}
 
-        def load_weights(tag):
-            weights.append(held([P, E * A * 2 * N], U8, "words", tag=tag))
+        def load_weights(e0, tag):
+            weights[e0] = held([P, 3 * A * 2 * N], U8, "words_%d" % e0, tag=tag)
             nc.sync.dma_start(
-                out=weights[0][:].bitcast(I32).rearrange("p (m c) -> p m c", c=N // 2),
-                in_=w_words.bitcast(I32).rearrange("e a p c -> p (e a) c"),
+                out=weights[e0][:].bitcast(I32).rearrange("p (m c) -> p m c", c=N // 2),
+                in_=w_words[e0 : e0 + 3].bitcast(I32).rearrange("e a p c -> p (e a) c"),
             )
 
         def multiply(a, block):
@@ -172,7 +172,7 @@ def tile_moe_rag_lin_bias_kernel(tc, xT, w_words, w_scales, b, gate, offs, pos1,
             m = e * A + a
             nc.tensor.matmul_mx(
                 out=banks[bank][:, 0:sn],
-                lhsT=weights[0][:, 2 * N * m : 2 * N * (m + 1)].bitcast(FP4X4),
+                lhsT=weights[e - e % 3][:, 2 * N * (m % (3 * A)) : 2 * N * (m % (3 * A) + 1)].bitcast(FP4X4),
                 lhsT_scale=wplane[:, N * m : N * (m + 1)],
                 rhs=slot_words(a, s0, sn).bitcast(FP8X4),
                 rhs_scale=slot_plane(a, s0, sn),
@@ -181,7 +181,7 @@ def tile_moe_rag_lin_bias_kernel(tc, xT, w_words, w_scales, b, gate, offs, pos1,
             )
 
         def leave(bank, e, s0, sn):
-            if s0 < 256:
+            if s0 < 384:
                 nc.vector.tensor_scalar_add(out=y[:, s0 : s0 + sn], in0=banks[bank][:, 0:sn], scalar1=b_t[:, e : e + 1])
             else:
                 nc.scalar.activation(out=y[:, s0 : s0 + sn], in_=banks[bank][:, 0:sn], func=IDENTITY, bias=b_t[:, e : e + 1])
@@ -192,7 +192,7 @@ def tile_moe_rag_lin_bias_kernel(tc, xT, w_words, w_scales, b, gate, offs, pos1,
             nc.sync.dma_start(
                 out=joined[PARKED + 4 * q : PARKED + 4 * q + 4, 0:T].bitcast(I32), in_=plane0[32 * q : 32 * q + 4, :].bitcast(I32)
             )
-        load_weights("grouped_0_512")
+        load_weights(3, "grouped_0_512")
         gather_words(gwords[0][:], 0, 0, S)
         cast(1)
         quantize(1)
@@ -206,6 +206,7 @@ def tile_moe_rag_lin_bias_kernel(tc, xT, w_words, w_scales, b, gate, offs, pos1,
         gather_words(gwords[2][:], 2, 0, S)
         cast(3)
         quantize(3)
+        load_weights(0, "grouped_3_512")
         cast(4)
         quantize(4)
         nc.vector.tensor_copy(out=joined[0:PARKED, 0:T].bitcast(I32), in_=packed[0:PARKED, :].bitcast(I32))

@@ -45,7 +45,7 @@ def tile_moe_rag_lin_bias_kernel(tc, xT, w_words, w_scales, b, gate, offs, pos1,
 
         uneven = ((0, 512), (512, 768))
         whole = ((0, T),)
-        loads = (uneven, whole, whole, whole, whole)
+        loads = (whole, whole, whole, whole, whole)
         raws = {}
         groups = {}
 
@@ -85,11 +85,11 @@ def tile_moe_rag_lin_bias_kernel(tc, xT, w_words, w_scales, b, gate, offs, pos1,
         nc.sync.dma_start(pos1_t[:], pos1)
         nc.sync.dma_start(pos2_t[:], pos2)
 
-        shares = ((320, 160), (0, 256), (0, 0), (0, 0), (64, 256))
+        shares = ((400, 0), (192, 0), (0, 0), (0, 0), (64, 256))
 
         def interleave(copy, a, part, c0, c1):
             t0 = uneven[part][0]
-            l0 = t0 if a == 0 else 0
+            l0 = 0
             copy(
                 out=groups[(a, t0)][:, c0 - t0 : c1 - t0, :].rearrange("p (c i) j -> p c j i", i=2),
                 in_=raws[(a, l0)][:, :, c0 - l0 : c1 - l0].rearrange("p j (c i) -> p c j i", i=2),

@@ -27,6 +27,7 @@ SHIFTED = 112
 PARKED = 112
 WIDE = 2048
 TAIL = 1280
+REST = 128
 
 
 def tile_moe_rag_lin_bias_kernel(tc, xT, w_words, w_scales, b, gate, offs, pos1, pos2, out):
@@ -85,7 +86,7 @@ def tile_moe_rag_lin_bias_kernel(tc, xT, w_words, w_scales, b, gate, offs, pos1,
         nc.sync.dma_start(pos1_t[:], pos1)
         nc.sync.dma_start(pos2_t[:], pos2)
 
-        shares = ((400, 0), (192, 0), (0, 0), (0, 0), (64, 256))
+        shares = ((272, 128), (32, 256), (0, 64), (0, 0), (160, 256))
 
         def interleave(copy, a, part, c0, c1):
             t0 = uneven[part][0]
@@ -129,14 +130,22 @@ def tile_moe_rag_lin_bias_kernel(tc, xT, w_words, w_scales, b, gate, offs, pos1,
             gather(dst, codes[:, first : first + window(s1 - s0)], s0, s1)
 
         gwords = {}
+        rests = {}
         for a in range(3):
             gwords[a] = held([P, S], U32, "gwords_%d" % a)
+
+        def gather_rest(a, s0, tag):
+            rests[(a, s0)] = held([P, REST], U32, "rest_%d_%d" % (a, s0), tag=tag)
+            gather_words(rests[(a, s0)][:], a, s0, s0 + REST)
+
         gbytes = held([P, S], U8, "gbytes")
         late = []
 
         def slot_words(a, s0, sn):
             if a >= 3:
                 return late[0][:, (a - 3) * S + s0 : (a - 3) * S + s0 + sn]
+            if (a, s0) in rests:
+                return rests[(a, s0)][:]
             return gwords[a][:, s0 : s0 + sn]
 
         def slot_plane(a, s0, sn):
@@ -193,23 +202,27 @@ def tile_moe_rag_lin_bias_kernel(tc, xT, w_words, w_scales, b, gate, offs, pos1,
                 out=joined[PARKED + 4 * q : PARKED + 4 * q + 4, 0:T].bitcast(I32), in_=plane0[32 * q : 32 * q + 4, :].bitcast(I32)
             )
         load_weights(3, "grouped_0_512")
-        gather_words(gwords[0][:], 0, 0, S)
+        gather_words(gwords[0][:, REST:], 0, REST, S)
         cast(1)
         quantize(1)
-        gather_words(gwords[1][:], 1, 0, S)
+        gather_rest(0, 0, "raw_1_0")
+        gather_words(gwords[1][:, REST:], 1, REST, S)
         cast(2)
         quantize(2)
+        gather_rest(1, 0, "raw_2_0")
         b_t = held([P, E], F32, "b_t", tag="grouped_2_0")
         nc.sync.dma_start(out=b_t[:], in_=b)
         for q in range(4):
             nc.sync.dma_start(out=wplane[32 * q : 32 * q + 4, :].bitcast(I32), in_=wstage[4 * q : 4 * q + 4, :].bitcast(I32))
-        gather_words(gwords[2][:], 2, 0, S)
+        gather_words(gwords[2][:, 2 * REST :], 2, 2 * REST, S)
         cast(3)
         quantize(3)
         load_weights(0, "grouped_3_512")
         cast(4)
         quantize(4)
+        gather_rest(2, REST, "raw_4_0")
         nc.vector.tensor_copy(out=joined[0:PARKED, 0:T].bitcast(I32), in_=packed[0:PARKED, :].bitcast(I32))
+        gather_rest(2, 0, "grouped_4_0")
 
         def shift(a, s0, s1):
             k = 4 * (a - 1)

@@ -77,13 +77,13 @@ def tile_moe_rag_lin_bias_kernel(tc, xT, w_words, w_scales, b, gate, offs, pos1,
             nc.vector.memset(moved[(a, s0)][:].bitcast(I32), 0)
 
         load(3)
+        nc.sync.dma_start(pos1_t[:], pos1)
         load(4)
         wstage = held([16, E * A * N], U8, "wstage")
         nc.sync.dma_start(
             out=wstage[:].bitcast(I32).rearrange("r (m c) -> r m c", m=E * A),
             in_=w_scales.bitcast(I32).rearrange("e a r c -> r (e a) c"),
         )
-        nc.sync.dma_start(pos1_t[:], pos1)
         nc.sync.dma_start(pos2_t[:], pos2)
 
         shares = ((272, 128), (32, 256), (0, 64), (0, 0), (160, 256))
@@ -197,10 +197,8 @@ def tile_moe_rag_lin_bias_kernel(tc, xT, w_words, w_scales, b, gate, offs, pos1,
 
         cast(0)
         quantize(0)
-        for q in range(4):
-            nc.sync.dma_start(
-                out=joined[PARKED + 4 * q : PARKED + 4 * q + 4, 0:T].bitcast(I32), in_=plane0[32 * q : 32 * q + 4, :].bitcast(I32)
-            )
+        for r in range(4):
+            nc.sync.dma_start(out=joined[PARKED + r : P : 4, 0:T].bitcast(I32), in_=plane0[r:P:32, :].bitcast(I32))
         load_weights(3, "grouped_0_512")
         gather_words(gwords[0][:, REST:], 0, REST, S)
         cast(1)
@@ -212,8 +210,8 @@ def tile_moe_rag_lin_bias_kernel(tc, xT, w_words, w_scales, b, gate, offs, pos1,
         gather_rest(1, 0, "raw_2_0")
         b_t = held([P, E], F32, "b_t", tag="grouped_2_0")
         nc.sync.dma_start(out=b_t[:], in_=b)
-        for q in range(4):
-            nc.sync.dma_start(out=wplane[32 * q : 32 * q + 4, :].bitcast(I32), in_=wstage[4 * q : 4 * q + 4, :].bitcast(I32))
+        for r in range(4):
+            nc.sync.dma_start(out=wplane[r:P:32, :].bitcast(I32), in_=wstage[r:16:4, :].bitcast(I32))
         gather_words(gwords[2][:, 2 * REST :], 2, 2 * REST, S)
         cast(3)
         quantize(3)
@@ -232,10 +230,8 @@ def tile_moe_rag_lin_bias_kernel(tc, xT, w_words, w_scales, b, gate, offs, pos1,
         shift(3, LAST, S)
         shift(4, LAST, S)
         gather(gbytes[:, 0:LAST], joined[:], 0, LAST)
-        for q in range(4):
-            nc.sync.dma_start(
-                out=moved[(0, 0)][32 * q : 32 * q + 4, :].bitcast(I32), in_=gbytes[PARKED + 4 * q : PARKED + 4 * q + 4, :].bitcast(I32)
-            )
+        for r in range(4):
+            nc.sync.dma_start(out=moved[(0, 0)][r:P:32, :].bitcast(I32), in_=gbytes[PARKED + r : P : 4, :].bitcast(I32))
         shift(2, 0, S)
         shift(3, 0, LAST)
         shift(4, 0, LAST)

@@ -176,17 +176,17 @@ def tile_moe_rag_lin_bias_kernel(tc, xT, w_words, w_scales, b, gate, offs, pos1,
                 in_=w_words[e0 : e0 + 3].bitcast(I32).rearrange("e a p c -> p (e a) c"),
             )
 
-        def multiply(a, block):
+        def multiply(a, block, spare=None):
             bank, e, s0, sn = block
             m = e * A + a
             nc.tensor.matmul_mx(
-                out=banks[bank][:, 0:sn],
+                out=(banks[bank] if spare is None else spare)[:, 0:sn],
                 lhsT=weights[e - e % 3][:, 2 * N * (m % (3 * A)) : 2 * N * (m % (3 * A) + 1)].bitcast(FP4X4),
                 lhsT_scale=wplane[:, N * m : N * (m + 1)],
                 rhs=slot_words(a, s0, sn).bitcast(FP8X4),
                 rhs_scale=slot_plane(a, s0, sn),
                 start=(a == 1),
-                stop=(a == (2 if s0 >= LAST else 4)),
+                stop=(spare is not None or a == (2 if s0 >= LAST else 4)),
             )
 
         def leave(bank, e, s0, sn):
@@ -241,7 +241,9 @@ def tile_moe_rag_lin_bias_kernel(tc, xT, w_words, w_scales, b, gate, offs, pos1,
         gather_words(late[0][:, LAST:S], 3, LAST, S)
         gather_words(late[0][:, S + LAST :], 4, LAST, S)
         gather_words(late[0][:, 0:LAST], 3, 0, LAST)
-        for blk in blocks:
+        multiply(1, blocks[0])
+        multiply(1, blocks[0], psum.tile([P, 512], F32, name="spare"))
+        for blk in blocks[1:]:
             multiply(1, blk)
         for a in (3, 4):
             multiply(a, blocks[0])

@@ -86,7 +86,7 @@ def tile_moe_rag_lin_bias_kernel(tc, xT, w_words, w_scales, b, gate, offs, pos1,
         )
         nc.sync.dma_start(pos2_t[:], pos2)
 
-        shares = ((272, 128), (32, 256), (0, 64), (0, 0), (160, 256))
+        shares = ((272, 128), (112, 112), (0, 64), (0, 64), (288, 128))
 
         def interleave(copy, a, part, c0, c1):
             t0 = uneven[part][0]
@@ -220,7 +220,7 @@ def tile_moe_rag_lin_bias_kernel(tc, xT, w_words, w_scales, b, gate, offs, pos1,
         quantize(4)
         gather_rest(2, REST, "raw_4_0")
         nc.vector.tensor_copy(out=joined[0:PARKED, 0:T].bitcast(I32), in_=packed[0:PARKED, :].bitcast(I32))
-        gather_rest(2, 0, "grouped_4_0")
+        gather_rest(2, 0, "grouped_4_512")
 
         def shift(a, s0, s1):
             k = 4 * (a - 1)

@@ -28,6 +28,7 @@ PARKED = 112
 WIDE = 2048
 TAIL = 1280
 REST = 128
+SEAM = 24 * 1024
 
 
 def tile_moe_rag_lin_bias_kernel(tc, xT, w_words, w_scales, b, gate, offs, pos1, pos2, out):
@@ -62,12 +63,10 @@ def tile_moe_rag_lin_bias_kernel(tc, xT, w_words, w_scales, b, gate, offs, pos1,
         load(1)
         load(2)
 
-        wplane = held([P, E * A * N], U8, "wplane")
         plane0 = held([P, T], U8, "plane0")
         packed = held([P, T], U8, "packed")
-        joined = shared.tile([P, WIDE], U8, name="joined", offset=8 * S - WIDE // 2, align_bytes=64)
+        joined = shared.tile([P, WIDE], U8, name="joined", offset=8 * S - 64, align_bytes=64)
         codes = held([P, A * T + TAIL], U32, "codes")
-        nc.gpsimd.memset(wplane[:].bitcast(I32), 0)
         nc.vector.memset(codes[:, A * T :].bitcast(I32), 0)
         nc.vector.memset(packed[:].bitcast(I32), 0)
         nc.vector.memset(joined[:, T:].bitcast(I32), 0)
@@ -77,13 +76,8 @@ def tile_moe_rag_lin_bias_kernel(tc, xT, w_words, w_scales, b, gate, offs, pos1,
             nc.vector.memset(moved[(a, s0)][:].bitcast(I32), 0)
 
         load(3)
-        nc.sync.dma_start(pos1_t[:], pos1)
         load(4)
-        wstage = held([16, E * A * N], U8, "wstage")
-        nc.sync.dma_start(
-            out=wstage[:].bitcast(I32).rearrange("r (m c) -> r m c", m=E * A),
-            in_=w_scales.bitcast(I32).rearrange("e a r c -> r (e a) c"),
-        )
+        nc.sync.dma_start(pos1_t[:], pos1)
         nc.sync.dma_start(pos2_t[:], pos2)
 
         shares = ((272, 128), (112, 112), (0, 64), (0, 64), (288, 128))
@@ -98,7 +92,10 @@ def tile_moe_rag_lin_bias_kernel(tc, xT, w_words, w_scales, b, gate, offs, pos1,
 
         def cast(a):
             for t0, t1 in uneven:
-                groups[(a, t0)] = held([P, t1 - t0, 4], BF16, "grouped_%d_%d" % (a, t0))
+                if a == 0 and t0:
+                    groups[(a, t0)] = shared.tile([P, t1 - t0, 4], BF16, name="grouped_0_short", offset=SEAM - 1024, align_bytes=64)
+                else:
+                    groups[(a, t0)] = held([P, t1 - t0, 4], BF16, "grouped_%d_%d" % (a, t0))
             for part, (t0, t1) in enumerate(uneven):
                 if t0 + shares[a][part] < t1:
                     interleave(nc.scalar.copy, a, part, t0 + shares[a][part], t1)
@@ -169,19 +166,22 @@ def tile_moe_rag_lin_bias_kernel(tc, xT, w_words, w_scales, b, gate, offs, pos1,
         y = held([P, S], F32, "y")
         weights = {}
 
-        def load_weights(e0, tag):
-            weights[e0] = held([P, 3 * A * 2 * N], U8, "words_%d" % e0, tag=tag)
+        def load_weights(e0, e1, words):
+            for e in range(e0, e1):
+                weights[e] = (words, e0)
             nc.sync.dma_start(
-                out=weights[e0][:].bitcast(I32).rearrange("p (m c) -> p m c", c=N // 2),
-                in_=w_words[e0 : e0 + 3].bitcast(I32).rearrange("e a p c -> p (e a) c"),
+                out=words[:].bitcast(I32).rearrange("p (m c) -> p m c", c=N // 2),
+                in_=w_words[e0:e1].bitcast(I32).rearrange("e a p c -> p (e a) c"),
             )
 
         def multiply(a, block, spare=None):
             bank, e, s0, sn = block
             m = e * A + a
+            words, e0 = weights[e]
+            i = m - e0 * A
             nc.tensor.matmul_mx(
                 out=(banks[bank] if spare is None else spare)[:, 0:sn],
-                lhsT=weights[e - e % 3][:, 2 * N * (m % (3 * A)) : 2 * N * (m % (3 * A) + 1)].bitcast(FP4X4),
+                lhsT=words[:, 2 * N * i : 2 * N * (i + 1)].bitcast(FP4X4),
                 lhsT_scale=wplane[:, N * m : N * (m + 1)],
                 rhs=slot_words(a, s0, sn).bitcast(FP8X4),
                 rhs_scale=slot_plane(a, s0, sn),
@@ -199,7 +199,14 @@ def tile_moe_rag_lin_bias_kernel(tc, xT, w_words, w_scales, b, gate, offs, pos1,
         quantize(0)
         for r in range(4):
             nc.sync.dma_start(out=joined[PARKED + r : P : 4, 0:T].bitcast(I32), in_=plane0[r:P:32, :].bitcast(I32))
-        load_weights(3, "grouped_0_512")
+        load_weights(3, 6, shared.tile([P, 3 * A * 2 * N], U8, name="words_3", offset=SEAM - 3 * A * 2 * N, align_bytes=64))
+        wplane = shared.tile([P, E * A * N], U8, name="wplane", offset=SEAM, align_bytes=64)
+        nc.gpsimd.memset(wplane[:].bitcast(I32), 0)
+        for r in range(4):
+            nc.sync.dma_start(
+                out=wplane[r:P:32, :].bitcast(I32).rearrange("q (m c) -> q m c", m=E * A),
+                in_=w_scales.bitcast(I32)[:, :, r:16:4, :].rearrange("e a q c -> q (e a) c"),
+            )
         gather_words(gwords[0][:, REST:], 0, REST, S)
         cast(1)
         quantize(1)
@@ -208,14 +215,10 @@ def tile_moe_rag_lin_bias_kernel(tc, xT, w_words, w_scales, b, gate, offs, pos1,
         cast(2)
         quantize(2)
         gather_rest(1, 0, "raw_2_0")
-        b_t = held([P, E], F32, "b_t", tag="grouped_2_0")
-        nc.sync.dma_start(out=b_t[:], in_=b)
-        for r in range(4):
-            nc.sync.dma_start(out=wplane[r:P:32, :].bitcast(I32), in_=wstage[r:16:4, :].bitcast(I32))
         gather_words(gwords[2][:, 2 * REST :], 2, 2 * REST, S)
         cast(3)
         quantize(3)
-        load_weights(0, "grouped_3_512")
+        load_weights(1, 3, held([P, 2 * A * 2 * N], U8, "words_1", tag="grouped_3_512"))
         cast(4)
         quantize(4)
         gather_rest(2, REST, "raw_4_0")
@@ -233,9 +236,12 @@ def tile_moe_rag_lin_bias_kernel(tc, xT, w_words, w_scales, b, gate, offs, pos1,
         for r in range(4):
             nc.sync.dma_start(out=moved[(0, 0)][r:P:32, :].bitcast(I32), in_=gbytes[PARKED + r : P : 4, :].bitcast(I32))
         shift(2, 0, S)
+        load_weights(0, 1, shared.tile([P, A * 2 * N], U8, name="words_0", offset=8 * S + 64, align_bytes=64))
         shift(3, 0, LAST)
         shift(4, 0, LAST)
-        gates = shared.tile([P, 2, T], F32, name="gates", offset=8 * S, align_bytes=64)
+        b_t = shared.tile([P, E], F32, name="b_t", offset=8 * S, align_bytes=64)
+        nc.sync.dma_start(out=b_t[:], in_=b)
+        gates = shared.tile([P, 2, T], F32, name="gates", offset=8 * S + 64 + A * 2 * N, align_bytes=64)
         nc.sync.dma_start(out=gates[:], in_=gate.rearrange("c p t -> p c t"))
         late.append(shared.tile([P, 2 * S], U32, name="late", offset=0, align_bytes=64))
         gather_words(late[0][:, LAST:S], 3, LAST, S)
@@ -243,14 +249,16 @@ def tile_moe_rag_lin_bias_kernel(tc, xT, w_words, w_scales, b, gate, offs, pos1,
         gather_words(late[0][:, 0:LAST], 3, 0, LAST)
         multiply(1, blocks[0])
         multiply(1, blocks[0], psum.tile([P, 512], F32, name="spare"))
-        for blk in blocks[1:]:
+        for blk in blocks[1:-1]:
             multiply(1, blk)
         for a in (3, 4):
             multiply(a, blocks[0])
         for a in (0, 2):
-            for blk in blocks:
+            for blk in blocks[:-1]:
                 multiply(a, blk)
         leave(*blocks[0])
+        for a in (1, 0, 2):
+            multiply(a, blocks[-1])
         for blk in blocks[1:]:
             multiply(3, blk)
         for s0, s1 in ((640, 1024), (384, 640), (128, 384), (0, 128)):

@@ -22,8 +22,8 @@ S = 1536
 E = 6
 N = 128
 A = 5
-LAST = 1024
-SHIFTED = 112
+LAST = 640
+SHIFTED = 100
 PARKED = 112
 WIDE = 2048
 TAIL = 1280
@@ -71,7 +71,7 @@ def tile_moe_rag_lin_bias_kernel(tc, xT, w_words, w_scales, b, gate, offs, pos1,
         nc.vector.memset(packed[:].bitcast(I32), 0)
         nc.vector.memset(joined[:, T:].bitcast(I32), 0)
         moved = {}
-        for a, s0, s1 in ((3, LAST, S), (4, LAST, S), (0, 0, S), (2, 0, S), (3, 0, LAST), (4, 0, LAST)):
+        for a, s0, s1 in ((2, LAST, S), (3, LAST, S), (0, 0, S), (4, 0, S), (2, 0, LAST), (3, 0, LAST)):
             moved[(a, s0)] = held([P, s1 - s0], U8, "moved_%d_%d" % (a, s0))
             nc.vector.memset(moved[(a, s0)][:].bitcast(I32), 0)
 
@@ -80,7 +80,7 @@ def tile_moe_rag_lin_bias_kernel(tc, xT, w_words, w_scales, b, gate, offs, pos1,
         nc.sync.dma_start(pos1_t[:], pos1)
         nc.sync.dma_start(pos2_t[:], pos2)
 
-        shares = ((272, 128), (112, 112), (0, 64), (0, 64), (288, 128))
+        shares = ((272, 128), (112, 112), (0, 64), (0, 64), (272, 128))
 
         def interleave(copy, a, part, c0, c1):
             t0 = uneven[part][0]
@@ -148,7 +148,7 @@ def tile_moe_rag_lin_bias_kernel(tc, xT, w_words, w_scales, b, gate, offs, pos1,
         def slot_plane(a, s0, sn):
             if a == 1:
                 return gbytes[:, s0 : s0 + sn]
-            p0 = LAST if a > 2 and s0 >= LAST else 0
+            p0 = LAST if a in (2, 3) and s0 >= LAST else 0
             return moved[(a, p0)][:, s0 - p0 : s0 - p0 + sn]
 
         blocks = [
@@ -186,7 +186,7 @@ def tile_moe_rag_lin_bias_kernel(tc, xT, w_words, w_scales, b, gate, offs, pos1,
                 rhs=slot_words(a, s0, sn).bitcast(FP8X4),
                 rhs_scale=slot_plane(a, s0, sn),
                 start=(a == 1),
-                stop=(spare is not None or a == (2 if s0 >= LAST else 4)),
+                stop=(spare is not None or a == (4 if s0 >= LAST else 3)),
             )
 
         def leave(bank, e, s0, sn):
@@ -229,16 +229,16 @@ def tile_moe_rag_lin_bias_kernel(tc, xT, w_words, w_scales, b, gate, offs, pos1,
             k = 4 * (a - 1)
             nc.sync.dma_start(out=moved[(a, s0)][0:SHIFTED, :].bitcast(I32), in_=gbytes[k : k + SHIFTED, s0:s1].bitcast(I32))
 
-        gather(gbytes[:, LAST:S], joined[:, 0:T], LAST, S)
+        gather(gbytes[:, LAST:S], joined[:], LAST, S)
+        shift(2, LAST, S)
         shift(3, LAST, S)
-        shift(4, LAST, S)
         gather(gbytes[:, 0:LAST], joined[:], 0, LAST)
         for r in range(4):
             nc.sync.dma_start(out=moved[(0, 0)][r:P:32, :].bitcast(I32), in_=gbytes[PARKED + r : P : 4, :].bitcast(I32))
-        shift(2, 0, S)
+        shift(4, 0, S)
+        shift(2, 0, LAST)
         load_weights(0, 1, shared.tile([P, A * 2 * N], U8, name="words_0", offset=8 * S + 64, align_bytes=64))
         shift(3, 0, LAST)
-        shift(4, 0, LAST)
         b_t = shared.tile([P, E], F32, name="b_t", offset=8 * S, align_bytes=64)
         nc.sync.dma_start(out=b_t[:], in_=b)
         gates = shared.tile([P, 2, T], F32, name="gates", offset=8 * S + 64 + A * 2 * N, align_bytes=64)
@@ -246,40 +246,55 @@ def tile_moe_rag_lin_bias_kernel(tc, xT, w_words, w_scales, b, gate, offs, pos1,
         late.append(shared.tile([P, 2 * S], U32, name="late", offset=0, align_bytes=64))
         gather_words(late[0][:, LAST:S], 3, LAST, S)
         gather_words(late[0][:, S + LAST :], 4, LAST, S)
-        gather_words(late[0][:, 0:LAST], 3, 0, LAST)
+        gather_words(late[0][:, S : S + LAST], 4, 0, LAST)
         multiply(1, blocks[0])
         multiply(1, blocks[0], psum.tile([P, 512], F32, name="spare"))
         for blk in blocks[1:-1]:
             multiply(1, blk)
-        for a in (3, 4):
-            multiply(a, blocks[0])
-        for a in (0, 2):
-            for blk in blocks[:-1]:
+        for a, some in ((2, blocks[:3]), (3, blocks[:3]), (0, blocks[:-1]), (4, blocks[:3]), (2, blocks[3:-1])):
+            for blk in some:
                 multiply(a, blk)
-        leave(*blocks[0])
-        for a in (1, 0, 2):
+        for blk in blocks[:3]:
+            leave(*blk)
+        for blk in blocks[3:-1]:
+            multiply(4, blk)
+        for a in (1, 0, 2, 4):
             multiply(a, blocks[-1])
-        for blk in blocks[1:]:
-            multiply(3, blk)
-        for s0, s1 in ((640, 1024), (384, 640), (128, 384), (0, 128)):
-            gather_words(late[0][:, S + s0 : S + s1], 4, s0, s1)
+        for s0, s1 in ((384, 640), (128, 384), (0, 128)):
+            gather_words(late[0][:, s0:s1], 3, s0, s1)
             for blk in blocks:
                 if s0 <= blk[2] < s1:
-                    multiply(4, blk)
+                    multiply(3, blk)
                     leave(*blk)
 
-        halves = ((0, 512), (512, T))
-        first, picked, second = {}, {}, {}
-        for t0, t1 in halves:
+        front, back = (0, 512), (512, T)
+        quarters = ((512, 640), (640, T))
+        picked = {}
+        for t0, t1 in (front, back):
             picked[t0] = held([P, t1 - t0], F32, "picked_%d" % t0)
             nc.scalar.activation(picked[t0][:], y[:].indirect(pos2_t[:, t0 // 16 : t1 // 16]), COPY)
-        for t0, t1 in halves:
+        first, second = {}, {}
+
+        def pick(t0, t1):
             first[t0] = held([P, t1 - t0], F32, "first_%d" % t0)
             nc.vector.tensor_tensor(first[t0][:], y[:].indirect(pos1_t[:, t0 // 16 : t1 // 16]), gates[:, 0, t0:t1], MULT)
-        for t0, t1 in halves:
+
+        def weigh(t0, t1, p0):
             second[t0] = held([P, t1 - t0], F32, "second_%d" % t0)
-            nc.vector.tensor_tensor(second[t0][:], picked[t0][:], gates[:, 1, t0:t1], MULT)
-        for t0, t1 in halves:
-            total = held([P, t1 - t0], F32, "total_%d" % t0)
-            nc.vector.tensor_add(out=total[:], in0=first[t0][:], in1=second[t0][:])
-            nc.sync.dma_start(out=out[:, t0:t1], in_=total[:])
+            nc.vector.tensor_tensor(second[t0][:], picked[p0][:, t0 - p0 : t1 - p0], gates[:, 1, t0:t1], MULT)
+
+        def add(total, t0):
+            nc.vector.tensor_add(out=total, in0=first[t0][:], in1=second[t0][:])
+
+        totals = [held([P, t1 - t0], F32, "total_%d" % t0) for t0, t1 in (front, back)]
+        pick(*front)
+        pick(*quarters[0])
+        weigh(*front, front[0])
+        pick(*quarters[1])
+        add(totals[0][:], front[0])
+        nc.sync.dma_start(out=out[:, front[0] : front[1]], in_=totals[0][:])
+        for t0, t1 in quarters:
+            weigh(t0, t1, back[0])
+        for t0, t1 in quarters:
+            add(totals[1][:, t0 - back[0] : t1 - back[0]], t0)
+        nc.sync.dma_start(out=out[:, back[0] : back[1]], in_=totals[1][:])

@@ -22,8 +22,7 @@ S = 1536
 E = 6
 N = 128
 A = 5
-LAST = 640
-SHIFTED = 100
+LAST = 1024
 PARKED = 112
 WIDE = 2048
 TAIL = 1280
@@ -71,16 +70,16 @@ def tile_moe_rag_lin_bias_kernel(tc, xT, w_words, w_scales, b, gate, offs, pos1,
         nc.vector.memset(packed[:].bitcast(I32), 0)
         nc.vector.memset(joined[:, T:].bitcast(I32), 0)
         moved = {}
-        for a, s0, s1 in ((2, LAST, S), (3, LAST, S), (0, 0, S), (4, 0, S), (2, 0, LAST), (3, 0, LAST)):
-            moved[(a, s0)] = held([P, s1 - s0], U8, "moved_%d_%d" % (a, s0))
-            nc.vector.memset(moved[(a, s0)][:].bitcast(I32), 0)
+        for a in (0, 2, 3, 4):
+            moved[a] = held([P, S], U8, "moved_%d" % a)
+            nc.vector.memset(moved[a][:].bitcast(I32), 0)
 
         load(3)
         load(4)
         nc.sync.dma_start(pos1_t[:], pos1)
         nc.sync.dma_start(pos2_t[:], pos2)
 
-        shares = ((272, 128), (112, 112), (0, 64), (0, 64), (272, 128))
+        shares = ((272, 128), (112, 112), (0, 64), (0, 64), (288, 128))
 
         def interleave(copy, a, part, c0, c1):
             t0 = uneven[part][0]
@@ -148,8 +147,7 @@ def tile_moe_rag_lin_bias_kernel(tc, xT, w_words, w_scales, b, gate, offs, pos1,
         def slot_plane(a, s0, sn):
             if a == 1:
                 return gbytes[:, s0 : s0 + sn]
-            p0 = LAST if a in (2, 3) and s0 >= LAST else 0
-            return moved[(a, p0)][:, s0 - p0 : s0 - p0 + sn]
+            return moved[a][:, s0 : s0 + sn]
 
         blocks = [
             (6, 5, 1024, 512),
@@ -186,7 +184,7 @@ def tile_moe_rag_lin_bias_kernel(tc, xT, w_words, w_scales, b, gate, offs, pos1,
                 rhs=slot_words(a, s0, sn).bitcast(FP8X4),
                 rhs_scale=slot_plane(a, s0, sn),
                 start=(a == 1),
-                stop=(spare is not None or a == (4 if s0 >= LAST else 3)),
+                stop=(spare is not None or a == 4),
             )
 
         def leave(bank, e, s0, sn):
@@ -225,76 +223,51 @@ def tile_moe_rag_lin_bias_kernel(tc, xT, w_words, w_scales, b, gate, offs, pos1,
         nc.vector.tensor_copy(out=joined[0:PARKED, 0:T].bitcast(I32), in_=packed[0:PARKED, :].bitcast(I32))
         gather_rest(2, 0, "grouped_4_512")
 
-        def shift(a, s0, s1):
-            k = 4 * (a - 1)
-            nc.sync.dma_start(out=moved[(a, s0)][0:SHIFTED, :].bitcast(I32), in_=gbytes[k : k + SHIFTED, s0:s1].bitcast(I32))
+        def lift(a):
+            for r in range(4):
+                rows = gbytes[PARKED + r : P : 4, :] if a == 0 else gbytes[4 * (a - 1) + r : 4 * (a - 1) + r + 97 : 32, :]
+                nc.sync.dma_start(out=moved[a][r:P:32, :].bitcast(I32), in_=rows.bitcast(I32))
 
         gather(gbytes[:, LAST:S], joined[:], LAST, S)
-        shift(2, LAST, S)
-        shift(3, LAST, S)
         gather(gbytes[:, 0:LAST], joined[:], 0, LAST)
-        for r in range(4):
-            nc.sync.dma_start(out=moved[(0, 0)][r:P:32, :].bitcast(I32), in_=gbytes[PARKED + r : P : 4, :].bitcast(I32))
-        shift(4, 0, S)
-        shift(2, 0, LAST)
+        for a in (0, 2, 3, 4):
+            lift(a)
         load_weights(0, 1, shared.tile([P, A * 2 * N], U8, name="words_0", offset=8 * S + 64, align_bytes=64))
-        shift(3, 0, LAST)
         b_t = shared.tile([P, E], F32, name="b_t", offset=8 * S, align_bytes=64)
         nc.sync.dma_start(out=b_t[:], in_=b)
         gates = shared.tile([P, 2, T], F32, name="gates", offset=8 * S + 64 + A * 2 * N, align_bytes=64)
         nc.sync.dma_start(out=gates[:], in_=gate.rearrange("c p t -> p c t"))
         late.append(shared.tile([P, 2 * S], U32, name="late", offset=0, align_bytes=64))
-        gather_words(late[0][:, LAST:S], 3, LAST, S)
-        gather_words(late[0][:, S + LAST :], 4, LAST, S)
-        gather_words(late[0][:, S : S + LAST], 4, 0, LAST)
+        gather_words(late[0][:, 0:S], 3, 0, S)
         multiply(1, blocks[0])
         multiply(1, blocks[0], psum.tile([P, 512], F32, name="spare"))
         for blk in blocks[1:-1]:
             multiply(1, blk)
-        for a, some in ((2, blocks[:3]), (3, blocks[:3]), (0, blocks[:-1]), (4, blocks[:3]), (2, blocks[3:-1])):
-            for blk in some:
+        for a in (0, 2, 3):
+            for blk in blocks[:-1]:
                 multiply(a, blk)
-        for blk in blocks[:3]:
-            leave(*blk)
-        for blk in blocks[3:-1]:
-            multiply(4, blk)
-        for a in (1, 0, 2, 4):
-            multiply(a, blocks[-1])
-        for s0, s1 in ((384, 640), (128, 384), (0, 128)):
-            gather_words(late[0][:, s0:s1], 3, s0, s1)
+        for s0, s1 in ((LAST, S), (640, LAST), (384, 640), (128, 384), (0, 128)):
+            gather_words(late[0][:, S + s0 : S + s1], 4, s0, s1)
+            if s0 == 128:
+                for a in (1, 0, 2, 3):
+                    multiply(a, blocks[-1])
             for blk in blocks:
                 if s0 <= blk[2] < s1:
-                    multiply(3, blk)
+                    multiply(4, blk)
                     leave(*blk)
 
         front, back = (0, 512), (512, T)
-        quarters = ((512, 640), (640, T))
-        picked = {}
+        picked, first, second = {}, {}, {}
         for t0, t1 in (front, back):
             picked[t0] = held([P, t1 - t0], F32, "picked_%d" % t0)
             nc.scalar.activation(picked[t0][:], y[:].indirect(pos2_t[:, t0 // 16 : t1 // 16]), COPY)
-        first, second = {}, {}
-
-        def pick(t0, t1):
+        for t0, t1 in (front, back):
             first[t0] = held([P, t1 - t0], F32, "first_%d" % t0)
             nc.vector.tensor_tensor(first[t0][:], y[:].indirect(pos1_t[:, t0 // 16 : t1 // 16]), gates[:, 0, t0:t1], MULT)
-
-        def weigh(t0, t1, p0):
+        for t0, t1 in (front, back):
             second[t0] = held([P, t1 - t0], F32, "second_%d" % t0)
-            nc.vector.tensor_tensor(second[t0][:], picked[p0][:, t0 - p0 : t1 - p0], gates[:, 1, t0:t1], MULT)
-
-        def add(total, t0):
-            nc.vector.tensor_add(out=total, in0=first[t0][:], in1=second[t0][:])
-
-        totals = [held([P, t1 - t0], F32, "total_%d" % t0) for t0, t1 in (front, back)]
-        pick(*front)
-        pick(*quarters[0])
-        weigh(*front, front[0])
-        pick(*quarters[1])
-        add(totals[0][:], front[0])
-        nc.sync.dma_start(out=out[:, front[0] : front[1]], in_=totals[0][:])
-        for t0, t1 in quarters:
-            weigh(t0, t1, back[0])
-        for t0, t1 in quarters:
-            add(totals[1][:, t0 - back[0] : t1 - back[0]], t0)
-        nc.sync.dma_start(out=out[:, back[0] : back[1]], in_=totals[1][:])
+            nc.vector.tensor_tensor(second[t0][:], picked[t0][:], gates[:, 1, t0:t1], MULT)
+        for t0, t1 in (front, back):
+            total = held([P, t1 - t0], F32, "total_%d" % t0)
+            nc.vector.tensor_add(out=total[:], in0=first[t0][:], in1=second[t0][:])
+            nc.sync.dma_start(out=out[:, t0:t1], in_=total[:])

@@ -256,18 +256,34 @@ def tile_moe_rag_lin_bias_kernel(tc, xT, w_words, w_scales, b, gate, offs, pos1,
                     multiply(4, blk)
                     leave(*blk)
 
-        front, back = (0, 512), (512, T)
+        thirds = ((0, 256), (256, 512), (512, T))
         picked, first, second = {}, {}, {}
-        for t0, t1 in (front, back):
-            picked[t0] = held([P, t1 - t0], F32, "picked_%d" % t0)
-            nc.scalar.activation(picked[t0][:], y[:].indirect(pos2_t[:, t0 // 16 : t1 // 16]), COPY)
-        for t0, t1 in (front, back):
+        for t0, t1 in ((0, 256), (256, T)):
+            some = held([P, t1 - t0], F32, "picked_%d" % t0)
+            nc.scalar.activation(some[:], y[:].indirect(pos2_t[:, t0 // 16 : t1 // 16]), COPY)
+            for u0, u1 in thirds:
+                if t0 <= u0 < t1:
+                    picked[u0] = some[:, u0 - t0 : u1 - t0]
+
+        def pick(t0, t1):
             first[t0] = held([P, t1 - t0], F32, "first_%d" % t0)
             nc.vector.tensor_tensor(first[t0][:], y[:].indirect(pos1_t[:, t0 // 16 : t1 // 16]), gates[:, 0, t0:t1], MULT)
-        for t0, t1 in (front, back):
+
+        def weigh(t0, t1):
             second[t0] = held([P, t1 - t0], F32, "second_%d" % t0)
-            nc.vector.tensor_tensor(second[t0][:], picked[t0][:], gates[:, 1, t0:t1], MULT)
-        for t0, t1 in (front, back):
+            nc.vector.tensor_tensor(second[t0][:], picked[t0], gates[:, 1, t0:t1], MULT)
+
+        def store(t0, t1):
             total = held([P, t1 - t0], F32, "total_%d" % t0)
             nc.vector.tensor_add(out=total[:], in0=first[t0][:], in1=second[t0][:])
             nc.sync.dma_start(out=out[:, t0:t1], in_=total[:])
+
+        pick(*thirds[0])
+        pick(*thirds[1])
+        weigh(*thirds[0])
+        pick(*thirds[2])
+        store(*thirds[0])
+        weigh(*thirds[1])
+        weigh(*thirds[2])
+        store(*thirds[1])
+        store(*thirds[2])

@@ -22,6 +22,7 @@ S = 1536
 E = 6
 N = 128
 A = 5
+STARTS = (0, 128, 256, 384, 640, 1024, S)
 LAST = 1024
 PARKED = 112
 WIDE = 2048
@@ -79,7 +80,7 @@ def tile_moe_rag_lin_bias_kernel(tc, xT, w_words, w_scales, b, gate, offs, pos1,
         nc.sync.dma_start(pos1_t[:], pos1)
         nc.sync.dma_start(pos2_t[:], pos2)
 
-        shares = ((272, 128), (112, 112), (0, 64), (0, 64), (288, 128))
+        shares = ((272, 128), (112, 112), (0, 64), (0, 64), (304, 128))
 
         def interleave(copy, a, part, c0, c1):
             t0 = uneven[part][0]
@@ -150,8 +151,8 @@ def tile_moe_rag_lin_bias_kernel(tc, xT, w_words, w_scales, b, gate, offs, pos1,
             return moved[a][:, s0 : s0 + sn]
 
         blocks = [
-            (6, 5, 1024, 512),
-            (5, 4, 768, 256),
+            (5, 5, 1024, 512),
+            (4, 4, 768, 256),
             (4, 4, 640, 128),
             (3, 3, 384, 256),
             (2, 2, 256, 128),
@@ -159,7 +160,7 @@ def tile_moe_rag_lin_bias_kernel(tc, xT, w_words, w_scales, b, gate, offs, pos1,
             (0, 0, 0, 128),
         ]
         banks = []
-        for i in range(7):
+        for i in range(6):
             banks.append(psum.tile([P, 512], F32, name="bank_%d" % i))
         y = held([P, S], F32, "y")
         weights = {}
@@ -178,17 +179,18 @@ def tile_moe_rag_lin_bias_kernel(tc, xT, w_words, w_scales, b, gate, offs, pos1,
             words, e0 = weights[e]
             i = m - e0 * A
             nc.tensor.matmul_mx(
-                out=(banks[bank] if spare is None else spare)[:, 0:sn],
+                out=(banks[bank] if spare is None else spare)[:, s0 - STARTS[e] : s0 - STARTS[e] + sn],
                 lhsT=words[:, 2 * N * i : 2 * N * (i + 1)].bitcast(FP4X4),
                 lhsT_scale=wplane[:, N * m : N * (m + 1)],
                 rhs=slot_words(a, s0, sn).bitcast(FP8X4),
                 rhs_scale=slot_plane(a, s0, sn),
-                start=(a == 1),
-                stop=(spare is not None or a == 4),
+                start=(a == 1 and s0 + sn == STARTS[e + 1]),
+                stop=(spare is not None or (a == 4 and s0 == STARTS[e])),
             )
 
-        def leave(bank, e, s0, sn):
-            if s0 < 384:
+        def leave(bank, e):
+            s0, sn = STARTS[e], STARTS[e + 1] - STARTS[e]
+            if 0 < s0 < 384:
                 nc.vector.tensor_scalar_add(out=y[:, s0 : s0 + sn], in0=banks[bank][:, 0:sn], scalar1=b_t[:, e : e + 1])
             else:
                 nc.scalar.activation(out=y[:, s0 : s0 + sn], in_=banks[bank][:, 0:sn], func=IDENTITY, bias=b_t[:, e : e + 1])
@@ -254,36 +256,18 @@ def tile_moe_rag_lin_bias_kernel(tc, xT, w_words, w_scales, b, gate, offs, pos1,
             for blk in blocks:
                 if s0 <= blk[2] < s1:
                     multiply(4, blk)
-                    leave(*blk)
+                    if blk[2] == STARTS[blk[1]]:
+                        leave(*blk[:2])
 
         thirds = ((0, 256), (256, 512), (512, T))
-        picked, first, second = {}, {}, {}
-        for t0, t1 in ((0, 256), (256, T)):
-            some = held([P, t1 - t0], F32, "picked_%d" % t0)
-            nc.scalar.activation(some[:], y[:].indirect(pos2_t[:, t0 // 16 : t1 // 16]), COPY)
-            for u0, u1 in thirds:
-                if t0 <= u0 < t1:
-                    picked[u0] = some[:, u0 - t0 : u1 - t0]
-
-        def pick(t0, t1):
-            first[t0] = held([P, t1 - t0], F32, "first_%d" % t0)
-            nc.vector.tensor_tensor(first[t0][:], y[:].indirect(pos1_t[:, t0 // 16 : t1 // 16]), gates[:, 0, t0:t1], MULT)
-
-        def weigh(t0, t1):
-            second[t0] = held([P, t1 - t0], F32, "second_%d" % t0)
-            nc.vector.tensor_tensor(second[t0][:], picked[t0], gates[:, 1, t0:t1], MULT)
-
-        def store(t0, t1):
+        first = held([P, T], F32, "first")
+        second = held([P, T], F32, "second")
+        nc.vector.tensor_tensor(first[:], y[:].indirect(pos1_t[:]), gates[:, 0, :], MULT)
+        for t0, t1 in ((0, 512), (512, T)):
+            picked = held([P, t1 - t0], F32, "picked_%d" % t0)
+            nc.scalar.activation(picked[:], y[:].indirect(pos2_t[:, t0 // 16 : t1 // 16]), COPY)
+            nc.vector.tensor_tensor(second[:, t0:t1], picked[:], gates[:, 1, t0:t1], MULT)
+        for t0, t1 in thirds:
             total = held([P, t1 - t0], F32, "total_%d" % t0)
-            nc.vector.tensor_add(out=total[:], in0=first[t0][:], in1=second[t0][:])
+            nc.vector.tensor_add(out=total[:], in0=first[:, t0:t1], in1=second[:, t0:t1])
             nc.sync.dma_start(out=out[:, t0:t1], in_=total[:])
-
-        pick(*thirds[0])
-        pick(*thirds[1])
-        weigh(*thirds[0])
-        pick(*thirds[2])
-        store(*thirds[0])
-        weigh(*thirds[1])
-        weigh(*thirds[2])
-        store(*thirds[1])
-        store(*thirds[2])

from contextlib import ExitStack

import concourse.mybir as mybir

FLOPS = 2 * 1536 * 2560 * 128

F32 = mybir.dt.float32
BF16 = mybir.dt.bfloat16
I32 = mybir.dt.int32
U32 = mybir.dt.uint32
U16 = mybir.dt.uint16
U8 = mybir.dt.uint8
FP8X4 = mybir.dt.float8_e4m3fn_x4
FP4X4 = mybir.dt.float4_e2m1fn_x4
MULT = mybir.AluOpType.mult
COPY = mybir.ActivationFunctionType.Copy
IDENTITY = mybir.ActivationFunctionType.Identity

P = 128
T = 768
S = 1536
E = 6
N = 128
A = 5
STARTS = (0, 128, 256, 384, 640, 1024, S)
LAST = 1024
PARKED = 112
WIDE = 2048
TAIL = 1280
REST = 128
SEAM = 24 * 1024


def tile_moe_rag_lin_bias_kernel(tc, xT, w_words, w_scales, b, gate, offs, pos1, pos2, out):
    nc = tc.nc
    with ExitStack() as ctx:
        pool = ctx.enter_context(tc.tile_pool(name="held", bufs=1))
        psum = ctx.enter_context(tc.psum_pool(name="psum", bufs=1))
        shared = ctx.enter_context(tc.tile_pool(name="shared", bufs=1))

        def held(shape, dtype, name, tag=None):
            return pool.tile(shape, dtype, name=name, tag=tag or name, align_bytes=64)

        offs_t = held([P, S // 16], U16, "offs_t")
        pos1_t = held([P, T // 16], U16, "pos1_t")
        pos2_t = held([P, T // 16], U16, "pos2_t")

        uneven = ((0, 512), (512, 768))
        whole = ((0, T),)
        loads = (whole, whole, whole, whole, whole)
        raws = {}
        groups = {}

        def load(a):
            rows = xT[512 * a : 512 * (a + 1), :].rearrange("(p j) w -> p j w", j=4)
            for t0, t1 in loads[a]:
                raw = held([P, 4, t1 - t0], F32, "raw_%d_%d" % (a, t0))
                nc.sync.dma_start(out=raw[:], in_=rows[:, :, t0:t1])
                raws[(a, t0)] = raw

        load(0)
        nc.sync.dma_start(offs_t[:], offs)
        load(1)
        load(2)

        plane0 = held([P, T], U8, "plane0")
        packed = held([P, T], U8, "packed")
        joined = shared.tile([P, WIDE], U8, name="joined", offset=8 * S - 64, align_bytes=64)
        codes = held([P, A * T + TAIL], U32, "codes")
        nc.vector.memset(codes[:, A * T :].bitcast(I32), 0)
        nc.vector.memset(packed[:].bitcast(I32), 0)
        nc.vector.memset(joined[:, T:].bitcast(I32), 0)
        moved = {}
        for a in (0, 2, 3, 4):
            moved[a] = held([P, S], U8, "moved_%d" % a)
            nc.vector.memset(moved[a][:].bitcast(I32), 0)

        load(3)
        load(4)
        nc.sync.dma_start(pos1_t[:], pos1)
        nc.sync.dma_start(pos2_t[:], pos2)

        shares = ((272, 128), (112, 112), (0, 64), (0, 64), (304, 128))

        def interleave(copy, a, part, c0, c1):
            t0 = uneven[part][0]
            l0 = 0
            copy(
                out=groups[(a, t0)][:, c0 - t0 : c1 - t0, :].rearrange("p (c i) j -> p c j i", i=2),
                in_=raws[(a, l0)][:, :, c0 - l0 : c1 - l0].rearrange("p j (c i) -> p c j i", i=2),
            )

        def cast(a):
            for t0, t1 in uneven:
                if a == 0 and t0:
                    groups[(a, t0)] = shared.tile([P, t1 - t0, 4], BF16, name="grouped_0_short", offset=SEAM - 1024, align_bytes=64)
                else:
                    groups[(a, t0)] = held([P, t1 - t0, 4], BF16, "grouped_%d_%d" % (a, t0))
            for part, (t0, t1) in enumerate(uneven):
                if t0 + shares[a][part] < t1:
                    interleave(nc.scalar.copy, a, part, t0 + shares[a][part], t1)
            for part in order(a):
                t0 = uneven[part][0]
                if shares[a][part]:
                    interleave(nc.vector.tensor_copy, a, part, t0, t0 + shares[a][part])

        def order(a):
            return (1, 0) if shares[a][1] == 256 else (0, 1)

        def quantize(a):
            for part in order(a):
                t0, t1 = uneven[part]
                nc.vector.quantize_mx(
                    out=codes[:, (A - 1 - a) * T + t0 : (A - 1 - a) * T + t1].bitcast(FP8X4),
                    scales=plane0[:, t0:t1] if a == 0 else packed[4 * (a - 1) : P, t0:t1],
                    in_=groups[(a, t0)][:].rearrange("p w j -> p (w j)"),
                )

        def gather(dst, src, s0, s1):
            nc.vector.tensor_copy(dst, src.indirect(offs_t[:, s0 // 16 : s1 // 16]))

        def window(n):
            return T if n <= 512 else 1024 if n <= 768 else WIDE

        def gather_words(dst, a, s0, s1):
            first = (A - 1 - a) * T
            gather(dst, codes[:, first : first + window(s1 - s0)], s0, s1)

        gwords = {}
        rests = {}
        for a in range(3):
            gwords[a] = held([P, S], U32, "gwords_%d" % a)

        def gather_rest(a, s0, tag):
            rests[(a, s0)] = held([P, REST], U32, "rest_%d_%d" % (a, s0), tag=tag)
            gather_words(rests[(a, s0)][:], a, s0, s0 + REST)

        gbytes = held([P, S], U8, "gbytes")
        late = []

        def slot_words(a, s0, sn):
            if a >= 3:
                return late[0][:, (a - 3) * S + s0 : (a - 3) * S + s0 + sn]
            if (a, s0) in rests:
                return rests[(a, s0)][:]
            return gwords[a][:, s0 : s0 + sn]

        def slot_plane(a, s0, sn):
            if a == 1:
                return gbytes[:, s0 : s0 + sn]
            return moved[a][:, s0 : s0 + sn]

        blocks = [
            (5, 5, 1024, 512),
            (4, 4, 768, 256),
            (4, 4, 640, 128),
            (3, 3, 384, 256),
            (2, 2, 256, 128),
            (1, 1, 128, 128),
            (0, 0, 0, 128),
        ]
        banks = []
        for i in range(6):
            banks.append(psum.tile([P, 512], F32, name="bank_%d" % i))
        y = held([P, S], F32, "y")
        weights = {}

        def load_weights(e0, e1, words):
            for e in range(e0, e1):
                weights[e] = (words, e0)
            nc.sync.dma_start(
                out=words[:].bitcast(I32).rearrange("p (m c) -> p m c", c=N // 2),
                in_=w_words[e0:e1].bitcast(I32).rearrange("e a p c -> p (e a) c"),
            )

        def multiply(a, block, spare=None):
            bank, e, s0, sn = block
            m = e * A + a
            words, e0 = weights[e]
            i = m - e0 * A
            nc.tensor.matmul_mx(
                out=(banks[bank] if spare is None else spare)[:, s0 - STARTS[e] : s0 - STARTS[e] + sn],
                lhsT=words[:, 2 * N * i : 2 * N * (i + 1)].bitcast(FP4X4),
                lhsT_scale=wplane[:, N * m : N * (m + 1)],
                rhs=slot_words(a, s0, sn).bitcast(FP8X4),
                rhs_scale=slot_plane(a, s0, sn),
                start=(a == 1 and s0 + sn == STARTS[e + 1]),
                stop=(spare is not None or (a == 4 and s0 == STARTS[e])),
            )

        def leave(bank, e):
            s0, sn = STARTS[e], STARTS[e + 1] - STARTS[e]
            if 0 < s0 < 384:
                nc.vector.tensor_scalar_add(out=y[:, s0 : s0 + sn], in0=banks[bank][:, 0:sn], scalar1=b_t[:, e : e + 1])
            else:
                nc.scalar.activation(out=y[:, s0 : s0 + sn], in_=banks[bank][:, 0:sn], func=IDENTITY, bias=b_t[:, e : e + 1])

        cast(0)
        quantize(0)
        for r in range(4):
            nc.sync.dma_start(out=joined[PARKED + r : P : 4, 0:T].bitcast(I32), in_=plane0[r:P:32, :].bitcast(I32))
        load_weights(3, 6, shared.tile([P, 3 * A * 2 * N], U8, name="words_3", offset=SEAM - 3 * A * 2 * N, align_bytes=64))
        wplane = shared.tile([P, E * A * N], U8, name="wplane", offset=SEAM, align_bytes=64)
        nc.gpsimd.memset(wplane[:].bitcast(I32), 0)
        for r in range(4):
            nc.sync.dma_start(
                out=wplane[r:P:32, :].bitcast(I32).rearrange("q (m c) -> q m c", m=E * A),
                in_=w_scales.bitcast(I32)[:, :, r:16:4, :].rearrange("e a q c -> q (e a) c"),
            )
        gather_words(gwords[0][:, REST:], 0, REST, S)
        cast(1)
        quantize(1)
        gather_rest(0, 0, "raw_1_0")
        gather_words(gwords[1][:, REST:], 1, REST, S)
        cast(2)
        quantize(2)
        gather_rest(1, 0, "raw_2_0")
        gather_words(gwords[2][:, 2 * REST :], 2, 2 * REST, S)
        cast(3)
        quantize(3)
        load_weights(1, 3, held([P, 2 * A * 2 * N], U8, "words_1", tag="grouped_3_512"))
        cast(4)
        quantize(4)
        gather_rest(2, REST, "raw_4_0")
        nc.vector.tensor_copy(out=joined[0:PARKED, 0:T].bitcast(I32), in_=packed[0:PARKED, :].bitcast(I32))
        gather_rest(2, 0, "grouped_4_512")

        def lift(a):
            for r in range(4):
                rows = gbytes[PARKED + r : P : 4, :] if a == 0 else gbytes[4 * (a - 1) + r : 4 * (a - 1) + r + 97 : 32, :]
                nc.sync.dma_start(out=moved[a][r:P:32, :].bitcast(I32), in_=rows.bitcast(I32))

        gather(gbytes[:, LAST:S], joined[:], LAST, S)
        gather(gbytes[:, 0:LAST], joined[:], 0, LAST)
        for a in (0, 2, 3, 4):
            lift(a)
        load_weights(0, 1, shared.tile([P, A * 2 * N], U8, name="words_0", offset=8 * S + 64, align_bytes=64))
        b_t = shared.tile([P, E], F32, name="b_t", offset=8 * S, align_bytes=64)
        nc.sync.dma_start(out=b_t[:], in_=b)
        gates = shared.tile([P, 2, T], F32, name="gates", offset=8 * S + 64 + A * 2 * N, align_bytes=64)
        nc.sync.dma_start(out=gates[:], in_=gate.rearrange("c p t -> p c t"))
        late.append(shared.tile([P, 2 * S], U32, name="late", offset=0, align_bytes=64))
        gather_words(late[0][:, 0:S], 3, 0, S)
        multiply(1, blocks[0])
        multiply(1, blocks[0], psum.tile([P, 512], F32, name="spare"))
        for blk in blocks[1:-1]:
            multiply(1, blk)
        for a in (0, 2, 3):
            for blk in blocks[:-1]:
                multiply(a, blk)
        for s0, s1 in ((LAST, S), (640, LAST), (384, 640), (128, 384), (0, 128)):
            gather_words(late[0][:, S + s0 : S + s1], 4, s0, s1)
            if s0 == 128:
                for a in (1, 0, 2, 3):
                    multiply(a, blocks[-1])
            for blk in blocks:
                if s0 <= blk[2] < s1:
                    multiply(4, blk)
                    if blk[2] == STARTS[blk[1]]:
                        leave(*blk[:2])

        thirds = ((0, 256), (256, 512), (512, T))
        first = held([P, T], F32, "first")
        second = held([P, T], F32, "second")
        nc.vector.tensor_tensor(first[:], y[:].indirect(pos1_t[:]), gates[:, 0, :], MULT)
        for t0, t1 in ((0, 512), (512, T)):
            picked = held([P, t1 - t0], F32, "picked_%d" % t0)
            nc.scalar.activation(picked[:], y[:].indirect(pos2_t[:, t0 // 16 : t1 // 16]), COPY)
            nc.vector.tensor_tensor(second[:, t0:t1], picked[:], gates[:, 1, t0:t1], MULT)
        for t0, t1 in thirds:
            total = held([P, t1 - t0], F32, "total_%d" % t0)
            nc.vector.tensor_add(out=total[:], in0=first[:, t0:t1], in1=second[:, t0:t1])
            nc.sync.dma_start(out=out[:, t0:t1], in_=total[:])
